import numpy as np
import ml_dtypes


def mxq(x, axis, fmt="e4m3"):
    dtype, down = {"e4m3": (ml_dtypes.float8_e4m3fn, 7), "e5m2": (ml_dtypes.float8_e5m2, 14)}[fmt]
    v = np.moveaxis(np.asarray(x, np.float32).astype(ml_dtypes.bfloat16).astype(np.float64), axis, -1)
    blocks = v.reshape(v.shape[:-1] + (-1, 32))
    amax = np.abs(blocks).max(-1, keepdims=True)
    byte = np.maximum(np.where(amax > 0, np.frexp(amax)[1] - 1 + 127, 0) - down, 1)
    scale = np.exp2(byte - 127.0)
    codes = (blocks / scale).astype(np.float32).astype(dtype).astype(np.float64)
    return np.moveaxis((codes * scale).reshape(v.shape), -1, axis)


WIDE = False


def mx_kscale(k):
    if not WIDE:
        return np.ones(k)
    levels = np.array([10, -10, 5, -5, 0])
    if k % 512:
        return np.exp2(np.random.permutation(np.resize(levels, k // 32))).repeat(32)
    a = np.empty((k // 512, 16))
    for p in range(k // 512):
        a[p, :8] = np.random.permutation(np.resize(levels, 8))
        for g in range(8):
            far = levels[np.abs(levels - a[p, g]) >= 10]
            a[p, g + 8] = far[np.random.randint(len(far))]
    return np.exp2(a.ravel()).repeat(32)


def f64(x):
    return np.asarray(x).astype(np.float64)


def striped(idx):
    return np.tile(idx.reshape(-1, 16).T, (8, 1)).astype(np.uint16)


def unstriped(offs):
    return offs[:16].T.reshape(-1).astype(np.int64)


E2M1 = np.array([0.0, 0.5, 1.0, 1.5, 2.0, 3.0, 4.0, 6.0, -0.0, -0.5, -1.0, -1.5, -2.0, -3.0, -4.0, -6.0])


def pack_weight(w, fmt):
    k, n = w.shape
    w = f64(np.asarray(w, np.float32).astype(ml_dtypes.bfloat16)).reshape(k // 32, 32, n)
    amax = np.abs(w).max(1)
    if fmt == "e4m3":
        byte = np.frexp(amax)[1] - 1 + 127 - 7
    else:
        mant, ex = np.frexp(amax / 6.0)
        byte = np.where(mant > 0.5, ex, ex - 1) + 127
    byte = np.clip(np.where(amax > 0, byte, 1), 1, 254)
    scaled = (w * np.exp2(127.0 - byte)[:, None, :]).reshape(k, n).astype(np.float32)
    by_word = np.ascontiguousarray(scaled.reshape(k // 512, 128, 4, n).transpose(0, 1, 3, 2))
    if fmt == "e4m3":
        words = by_word.astype(ml_dtypes.float8_e4m3fn).view(np.uint8)
    else:
        c = by_word.astype(ml_dtypes.float4_e2m1fn).view(np.uint8) & 0xF
        words = (c[..., 0::2] | (c[..., 1::2] << 4)).reshape(k // 512, 128, 2 * n)
    return np.ascontiguousarray(words), np.ascontiguousarray(byte.astype(np.uint8).reshape(k // 512, 16, n))


def unpack_weight(words, scales, fmt):
    g, _, n = scales.shape
    words = np.ascontiguousarray(words).reshape(g, 128, n, -1)
    if fmt == "e4m3":
        vals = words.view(ml_dtypes.float8_e4m3fn).astype(np.float64)
    else:
        nib = np.empty((g, 128, n, 4), np.uint8)
        nib[..., 0::2] = words & 0xF
        nib[..., 1::2] = words >> 4
        vals = E2M1[nib]
    vals = vals * np.repeat(np.exp2(scales.astype(np.float64) - 127.0), 8, axis=1)[..., None]
    return vals.transpose(0, 1, 3, 2).reshape(g * 512, n)


def gelu(v):
    return 0.5 * v * (1.0 + np.tanh(np.sqrt(2.0 / np.pi) * (v + 0.044715 * v**3)))


def bf(x):
    return np.asarray(x, np.float32).astype(ml_dtypes.bfloat16)


def planes(Y):
    n, m = Y.shape
    b = f64(bf(Y)).reshape(n // 32, 32, m)
    amax = np.abs(b).max(1)
    byte = np.clip(np.where(amax > 0, np.frexp(amax)[1] - 1 + 127 - 7, 1), 1, 254)
    codes = (b * np.exp2(127.0 - byte)[:, None, :]).reshape(n, m).astype(np.float32).astype(ml_dtypes.float8_e4m3fn).view(np.uint8)
    words = codes.reshape(n // 512, 128, 4, m).transpose(0, 1, 3, 2)
    return np.ascontiguousarray(words), np.ascontiguousarray(byte.astype(np.uint8).reshape(n // 512, 16, m))


K, T, S, H, T2, P, N = 1024, 4096, 1024, 512, 2048, 1024, 384

def setup_inputs():
    n = np.random.standard_normal
    s, u = mx_kscale(K)[:, None], mx_kscale(H)[:, None]
    d = {}
    d["tab_words"], d["tab_scales"] = pack_weight(n((K, T)) * s, "e4m3")
    d["offs"] = striped(np.random.permutation(T)[:S])
    d["offs2"] = striped(np.random.permutation(T2)[:S])
    d["offs3"] = striped(np.random.permutation(T2)[:P])
    d["w1"] = (1.2 * n((K, H)) / K ** 0.5 / s).astype(np.float32)
    d["w2_words"], d["w2_scales"] = pack_weight(1.2 * n((K, H)) / K ** 0.5 / s * u.T, "e2m1")
    d["w3_words"], d["w3_scales"] = pack_weight(0.8 * n((K, H)) / K ** 0.5 / s * u.T, "e4m3")
    d["hum"] = n((H, S)).astype(np.float32)
    d["wgs"] = np.exp(0.3 * n((128, S))).astype(np.float32)
    d["page0"] = (n((H, T2)) * u).astype(np.float32)
    d["base"] = (0.5 * n(H) * u[:, 0]).astype(np.float32)
    d["w4"] = (4.0 * n((H, N)) / H ** 0.5 / u).astype(np.float32)
    return d

def reference(tab_words, tab_scales, offs, offs2, offs3, w1, w2_words, w2_scales,
              w3_words, w3_scales, hum, wgs, page0, base, w4):
    v = unpack_weight(tab_words, tab_scales, "e4m3")[:, unstriped(offs)]
    w2 = unpack_weight(w2_words, w2_scales, "e2m1")
    w3 = unpack_weight(w3_words, w3_scales, "e4m3")
    t = np.tanh((mxq(f64(w1), 0, "e4m3").T @ v) + f64(hum))
    h = t * (w2.T @ v) - (w3.T @ v)
    page = f64(page0).copy()
    page[:, unstriped(offs2)] = np.tile(f64(wgs), (H // 128, 1)) * h
    x = np.maximum(page[:, unstriped(offs3)], f64(base)[:, None])
    y = np.sqrt(1.0 + np.abs(mxq(f64(w4), 0, "e4m3").T @ mxq(x, 0, "e4m3")))
    words, scales = planes(page)
    return y, page, words, scales

@@ -1,0 +1,297 @@
+from contextlib import ExitStack
+
+import concourse.mybir as mybir
+
+K, T, S, H, T2, NREAD, N = 1024, 4096, 1024, 512, 2048, 1024, 384
+FLOPS = 2 * (3 * K * H * S + H * N * NREAD)
+
+F32 = mybir.dt.float32
+BF16 = mybir.dt.bfloat16
+I32 = mybir.dt.int32
+U32 = mybir.dt.uint32
+U16 = mybir.dt.uint16
+U8 = mybir.dt.uint8
+FP8X4 = mybir.dt.float8_e4m3fn_x4
+FP4X4 = mybir.dt.float4_e2m1fn_x4
+ALU = mybir.AluOpType
+ACT = mybir.ActivationFunctionType
+
+P = 128
+PACK = 4
+PASSES = K // (P * PACK)
+BANK = 512
+HALVES = S // BANK
+UNITS = PACK * HALVES
+CHUNKS = T2 // BANK
+LIST_COLS = BANK // 16
+W1_SPLIT = 84
+
+
+def tile_list_arrester_varistor_page_kernel(
+    tc, tab_words, tab_scales, offs, offs2, offs3, w1, w2_words, w2_scales,
+    w3_words, w3_scales, hum, wgs, page0, base, w4, out_0, out_1, out_2, out_3,
+):
+    nc = tc.nc
+    hum_rows = hum.rearrange("(p t) j -> t p j", t=PACK)
+    wgs_rows = wgs.rearrange("(q t) j -> t q j", t=PACK)
+    page_in = page0.rearrange("(p t) c -> t p c", t=PACK)
+    page_out = out_1.rearrange("(p t) c -> t p c", t=PACK)
+
+    with ExitStack() as ctx:
+        lists = ctx.enter_context(tc.tile_pool(name="lists", bufs=1))
+        keep = ctx.enter_context(tc.tile_pool(name="keep", bufs=1))
+        ring = ctx.enter_context(tc.tile_pool(name="ring", bufs=3))
+        psum = ctx.enter_context(tc.psum_pool(name="psum", bufs=2))
+
+        idx1 = lists.tile([P, S // 16], U16, name="idx1")
+        idx2 = lists.tile([P, S // 16], U16, name="idx2")
+        idx3 = lists.tile([P, NREAD // 16], U16, name="idx3")
+
+        planes = keep.tile([P, PASSES, S + 2 * H], U8, name="planes", align_bytes=64)
+        picked = [[keep.tile([P, BANK], I32, name="picked_%d_%d" % (a, h), align_bytes=64) for h in range(HALVES)] for a in range(PASSES)]
+        w1_codes = [keep.tile([P, H], U32, name="w1_codes_%d" % a, align_bytes=64) for a in range(PASSES)]
+        w1_scales = [keep.tile([P, H], U8, name="w1_scales_%d" % a, align_bytes=64) for a in range(PASSES)]
+        w2_dealt = keep.tile([P, PASSES, PACK, 2 * P], U8, name="w2_dealt", align_bytes=64)
+        w3_dealt = keep.tile([P, PASSES, PACK, P], I32, name="w3_dealt", align_bytes=64)
+        hum_sb = [keep.tile([P, BANK], F32, name="hum_%d" % u, tag="unit_%d" % u) for u in range(UNITS)]
+        wgs_sb = [keep.tile([P, S], F32, name="wgs_%d" % t, tag="wgs_%d" % t) for t in range(PACK)]
+        page = [keep.tile([P, T2], F32, name="page_%d" % t) for t in range(PACK)]
+        base_sb = keep.tile([P, PACK], F32, name="base_sb")
+        w4_raw = keep.tile([P, PACK, N], F32, name="w4_raw")
+        w4_bf = keep.tile([P, N, PACK], BF16, name="w4_bf", align_bytes=64)
+        w4_codes = keep.tile([P, N], U32, name="w4_codes", align_bytes=64)
+        w4_scales = keep.tile([P, N], U8, name="w4_scales", align_bytes=64)
+
+        def load_wgs(t, cols):
+            for quad in range(4):
+                nc.sync.dma_start(out=wgs_sb[t][32 * quad:32 * quad + 32, cols], in_=wgs_rows[t][:, cols])
+
+        def load_hum(u):
+            t, h = divmod(u, HALVES)
+            nc.sync.dma_start(out=hum_sb[u][:], in_=hum_rows[t][:, BANK * h:BANK * (h + 1)])
+
+        warm = keep.tile([P, 2], F32, name="warm")
+        nc.vector.memset(warm[:, 0:1], 0.0)
+        nc.scalar.activation(warm[:, 1:2], warm[:, 0:1], ACT.Tanh)
+
+        with tc.tile_pool(name="head", bufs=1) as head:
+            table = [head.tile([P, T], I32, name="table_%d" % a) for a in range(PASSES)]
+            tab_rows = head.tile([P, T], U8, name="tab_rows")
+            picked_rows = head.tile([P, S], U8, name="picked_rows")
+            w_rows = head.tile([P, 2, H], U8, name="w_rows")
+            staged = head.tile([P, S + 2 * H], U8, name="staged")
+            w1_raw = [head.tile([P, PACK, H], F32, name="w1_raw_%d" % a) for a in range(PASSES)]
+            w1_bf = [head.tile([P, PACK, P, PACK], BF16, name="w1_bf_%d" % a, align_bytes=64) for a in range(PASSES)]
+            w2_raw = head.tile([P, PASSES, 2 * H], U8, name="w2_raw")
+            w3_raw = head.tile([P, PASSES, H], I32, name="w3_raw")
+
+            for lo, hi in ((32, 64), (64, 128)):
+                nc.vector.memset(tab_rows[lo:hi, :].bitcast(I32), 0)
+                nc.vector.memset(w_rows[lo:hi].rearrange("p w c -> p (w c)").bitcast(I32), 0)
+            nc.vector.memset(planes[:].rearrange("p a c -> p (a c)").bitcast(I32), 0)
+
+            nc.sync.dma_start(idx1[:], offs)
+            nc.sync.dma_start(out=tab_rows[0:32, :].bitcast(I32), in_=tab_scales.rearrange("a q n -> (a q) n").bitcast(I32))
+            for w, scales in enumerate((w2_scales, w3_scales)):
+                nc.sync.dma_start(out=w_rows[0:32, w, :].bitcast(I32), in_=scales.rearrange("a q c -> (a q) c").bitcast(I32))
+
+            def load_table(a):
+                nc.sync.dma_start(out=table[a][:], in_=tab_words[a].rearrange("p n i -> p (n i)").bitcast(I32))
+
+            for a in range(PASSES):
+                load_table(a)
+            for a in range(PASSES):
+                nc.sync.dma_start(out=w1_raw[a][:], in_=w1[512 * a:512 * a + 512, :].rearrange("(p j) c -> p j c", j=PACK))
+            load_hum(0)
+            nc.sync.dma_start(out=w2_raw[:].bitcast(I32), in_=w2_words.rearrange("a p c -> p a c").bitcast(I32))
+            nc.sync.dma_start(out=w3_raw[:], in_=w3_words.rearrange("a p c i -> p a (c i)").bitcast(I32))
+            load_hum(1)
+            load_wgs(0, slice(0, BANK))
+            nc.sync.dma_start(idx2[:], offs2)
+            nc.sync.dma_start(out=page[0][:], in_=page_in[0])
+            load_hum(2)
+            load_wgs(0, slice(BANK, S))
+            nc.sync.dma_start(idx3[:], offs3)
+            nc.sync.dma_start(out=base_sb[:], in_=base.rearrange("(p t) -> p t", t=PACK))
+            for t in range(1, PACK):
+                load_hum(2 * t + 1)
+                load_wgs(t, slice(0, S))
+                nc.sync.dma_start(out=page[t][:], in_=page_in[t])
+                if t + 1 < PACK:
+                    load_hum(2 * t + 2)
+            nc.sync.dma_start(out=w4_raw[:], in_=w4.rearrange("(p j) n -> p j n", j=PACK))
+
+            nc.vector.tensor_copy(picked_rows[:], tab_rows[:].indirect(idx1[:]))
+            nc.vector.tensor_copy(staged[:, 0:S].bitcast(I32), picked_rows[:].bitcast(I32))
+            nc.vector.tensor_copy(
+                staged[:, S:].rearrange("p (w t m) -> p w t m", w=2, t=PACK),
+                w_rows[:].rearrange("p w (m t) -> p w t m", t=PACK),
+            )
+            for a in range(PASSES):
+                for quad in range(4):
+                    row = 16 * a + 4 * quad
+                    nc.gpsimd.dma_start(
+                        out=planes[32 * quad:32 * quad + 4, a, :].bitcast(I32),
+                        in_=staged[row:row + 4, :].bitcast(I32),
+                    )
+
+            def pick(a, h):
+                nc.vector.tensor_copy(
+                    picked[a][h][:].bitcast(U32),
+                    table[a][:].bitcast(U32).indirect(idx1[:, LIST_COLS * h:LIST_COLS * (h + 1)]),
+                )
+
+            for a in range(PASSES):
+                for h in range(HALVES):
+                    pick(a, h)
+            for a in range(PASSES):
+                dealt = w1_bf[a][:].rearrange("p t m j -> p m t j")
+                raw = w1_raw[a][:].rearrange("p j (m t) -> p m t j", t=PACK)
+                nc.vector.tensor_copy(dealt[:, :W1_SPLIT], raw[:, :W1_SPLIT])
+                nc.scalar.copy(dealt[:, W1_SPLIT:], raw[:, W1_SPLIT:])
+                nc.vector.quantize_mx(
+                    out=w1_codes[a][:].bitcast(FP8X4), scales=w1_scales[a][:],
+                    in_=w1_bf[a][:].rearrange("p t m j -> p (t m j)"),
+                )
+            nc.vector.tensor_copy(
+                w2_dealt[:].rearrange("p a t (m e) -> p a t m e", e=2),
+                w2_raw[:].rearrange("p a (m t e) -> p a t m e", t=PACK, e=2),
+            )
+            nc.vector.tensor_copy(
+                w3_dealt[:].rearrange("p a t m -> p a m t"),
+                w3_raw[:].rearrange("p a (m t) -> p a m t", t=PACK),
+            )
+
+        tail = ctx.enter_context(tc.tile_pool(name="tail", bufs=1))
+        page_pairs = [tail.tile([P, 2, BANK, 2], BF16, name="page_pairs_%d" % c) for c in range(CHUNKS)]
+        x_pairs = [tail.tile([P, 2, BANK, 2], BF16, name="x_pairs_%d" % h) for h in range(HALVES)]
+        page_codes = tail.tile([P, T2], I32, name="page_codes", align_bytes=64)
+        page_scales = tail.tile([P, T2], U8, name="page_scales", align_bytes=64)
+
+        read = [[tail.tile([P, BANK], F32, name="read_%d_%d" % (t, h)) for h in range(HALVES)] for t in range(PACK)]
+        sums, tanh_of, third, prod = {}, {}, {}, {}
+
+        def products(u):
+            t, h = divmod(u, HALVES)
+            cols = slice(P * t, P * (t + 1))
+            banks = []
+            for w in range(3):
+                bank = psum.tile([P, BANK], F32, name="bank_%d" % w)
+                for a in range(PASSES):
+                    if w == 0:
+                        codes, scales = w1_codes[a][:, cols].bitcast(FP8X4), w1_scales[a][:, cols]
+                    elif w == 1:
+                        codes, scales = w2_dealt[:, a, t, :].bitcast(FP4X4), planes[:, a, S + P * t:S + P * (t + 1)]
+                    else:
+                        codes, scales = w3_dealt[:, a, t, :].bitcast(FP8X4), planes[:, a, S + H + P * t:S + H + P * (t + 1)]
+                    nc.tensor.matmul_mx(
+                        out=bank[:], lhsT=codes, lhsT_scale=scales,
+                        rhs=picked[a][h][:].bitcast(FP8X4), rhs_scale=planes[:, a, BANK * h:BANK * (h + 1)],
+                        start=(a == 0), stop=(a == PASSES - 1),
+                    )
+                banks.append(bank)
+            sums[u] = banks
+
+        def front(u):
+            t, h = divmod(u, HALVES)
+            cols = slice(BANK * h, BANK * (h + 1))
+            pre = ring.tile([P, BANK], F32, name="pre")
+            if u == 0:
+                nc.vector.tensor_tensor(pre[:], sums[u][0][:], hum_sb[u][:], ALU.add)
+            else:
+                nc.scalar.copy(pre[:], sums[u][0][:])
+                nc.gpsimd.tensor_tensor(pre[:], pre[:], hum_sb[u][:], ALU.add)
+                third[u] = ring.tile([P, BANK], F32, name="third")
+                nc.scalar.copy(third[u][:], sums[u][2][:])
+            tanh_of[u] = ring.tile([P, BANK], F32, name="tanh_of")
+            nc.scalar.activation(tanh_of[u][:], pre[:], ACT.Tanh)
+            prod[u] = ring.tile([P, BANK], F32, name="prod")
+            nc.vector.tensor_tensor(prod[u][:], sums[u][1][:], tanh_of[u][:], ALU.mult)
+
+        def back(u):
+            t, h = divmod(u, HALVES)
+            cols = slice(BANK * h, BANK * (h + 1))
+            slot = "unit_%d" % (u + 1) if 0 < u < UNITS - 1 else "cells_%d" % u
+            cells = keep.tile([P, BANK], F32, name="cells_%d" % u, tag=slot)
+            if u == 0:
+                nc.vector.tensor_tensor(prod[u][:], prod[u][:], sums[u][2][:], ALU.subtract)
+                nc.vector.tensor_tensor(cells[:], prod[u][:], wgs_sb[t][:, cols], ALU.mult)
+            else:
+                nc.gpsimd.tensor_tensor(prod[u][:], prod[u][:], third[u][:], ALU.subtract)
+                nc.gpsimd.tensor_tensor(cells[:], prod[u][:], wgs_sb[t][:, cols], ALU.mult)
+            nc.vector.tensor_copy(page[t][:].indirect(idx2[:, LIST_COLS * h:LIST_COLS * (h + 1)]), cells[:])
+
+        def read_page(t):
+            nc.sync.dma_start(out=page_out[t], in_=page[t][:])
+            for h in range(HALVES):
+                nc.vector.tensor_copy(read[t][h][:], page[t][:].indirect(idx3[:, LIST_COLS * h:LIST_COLS * (h + 1)]))
+
+        def floor_at_base(t, h):
+            nc.vector.tensor_scalar(x_pairs[h][:, t // 2, :, t % 2], read[t][h][:], late_base[:, t:t + 1], None, ALU.max)
+
+        def round_page(t):
+            for c in range(CHUNKS):
+                nc.scalar.copy(page_pairs[c][:, t // 2, :, t % 2], page[t][:, BANK * c:BANK * (c + 1)])
+
+        def weave(pairs):
+            woven = ring.tile([P, BANK * PACK], BF16, name="woven", align_bytes=64, bufs=2)
+            nc.vector.tensor_copy(
+                woven[:].bitcast(I32).rearrange("p (j u) -> p j u", u=2),
+                pairs[:].rearrange("p u j e -> p u (j e)").bitcast(I32).rearrange("p u j -> p j u"),
+            )
+            return woven
+
+        products(0)
+        front(0)
+        for u in range(UNITS):
+            if u + 1 < UNITS:
+                products(u + 1)
+                front(u + 1)
+            back(u)
+            if u % HALVES == HALVES - 1:
+                read_page(u // HALVES)
+            if u % HALVES == 0 and u > 0:
+                round_page(u // HALVES - 1)
+
+        nc.scalar.activation(warm[:, 1:2], tanh_of[UNITS - 1][:, 0:1], ACT.Sqrt, bias=1.0, scale=0.0)
+        nc.scalar.copy(w4_bf[:], w4_raw[:].rearrange("p j n -> p n j"))
+        for lo, hi in ((0, 256), (256, N)):
+            nc.vector.quantize_mx(
+                out=w4_codes[:, lo:hi].bitcast(FP8X4), scales=w4_scales[:, lo:hi],
+                in_=w4_bf[:, lo:hi, :].rearrange("p n j -> p (n j)"),
+            )
+        round_page(PACK - 1)
+        late_base = keep.tile([P, PACK], F32, name="late_base", tag="wgs_%d" % (PACK - 1))
+        nc.gpsimd.tensor_copy(late_base[:], base_sb[:])
+
+        for h in range(HALVES):
+            for t in range(PACK):
+                floor_at_base(t, h)
+            woven = weave(x_pairs[h])
+            x_codes = ring.tile([P, BANK], U32, name="x_codes", align_bytes=64, bufs=2)
+            x_scales = ring.tile([P, BANK], U8, name="x_scales", align_bytes=64, bufs=2)
+            nc.vector.quantize_mx(out=x_codes[:].bitcast(FP8X4), scales=x_scales[:], in_=woven[:])
+            for n in range(N // P):
+                cols = slice(P * n, P * (n + 1))
+                score = psum.tile([P, BANK], F32, name="bank_%d" % n)
+                nc.tensor.matmul_mx(
+                    out=score[:], lhsT=w4_codes[:, cols].bitcast(FP8X4), lhsT_scale=w4_scales[:, cols],
+                    rhs=x_codes[:].bitcast(FP8X4), rhs_scale=x_scales[:], start=True, stop=True,
+                )
+                size = ring.tile([P, BANK], F32, name="pre")
+                nc.scalar.activation(size[:], score[:], ACT.Abs)
+                root = tail.tile([P, BANK], F32, name="root_%d_%d" % (h, n))
+                nc.scalar.activation(root[:], size[:], ACT.Sqrt, bias=1.0)
+                nc.sync.dma_start(out=out_0[cols, BANK * h:BANK * (h + 1)], in_=root[:])
+
+        words_out = out_2[0].rearrange("p m i -> p (m i)").bitcast(I32)
+        for c in range(CHUNKS):
+            cols = slice(BANK * c, BANK * (c + 1))
+            woven = weave(page_pairs[c])
+            nc.vector.quantize_mx(out=page_codes[:, cols].bitcast(FP8X4), scales=page_scales[:, cols], in_=woven[:])
+            nc.sync.dma_start(out=words_out[:, cols], in_=page_codes[:, cols])
+        for quad in range(4):
+            nc.sync.dma_start(
+                out=out_3[0, 4 * quad:4 * quad + 4, :].bitcast(I32),
+                in_=page_scales[32 * quad:32 * quad + 4, :].bitcast(I32),
+            )

@@ -24,7 +24,8 @@ HALVES = S // BANK
 UNITS = PACK * HALVES
 CHUNKS = T2 // BANK
 LIST_COLS = BANK // 16
-W1_SPLIT = 84
+F32_MAX = 3.4028234663852886e38
+W1_SPLIT = ((0, 40), (64, 42))
 
 
 def tile_list_arrester_varistor_page_kernel(
@@ -35,6 +36,7 @@ def tile_list_arrester_varistor_page_kernel(
     hum_rows = hum.rearrange("(p t) j -> t p j", t=PACK)
     wgs_rows = wgs.rearrange("(q t) j -> t q j", t=PACK)
     page_in = page0.rearrange("(p t) c -> t p c", t=PACK)
+    scores_out = out_0.rearrange("(n p) m -> p n m", p=P)
     page_out = out_1.rearrange("(p t) c -> t p c", t=PACK)
 
     with ExitStack() as ctx:
@@ -54,12 +56,11 @@ def tile_list_arrester_varistor_page_kernel(
         w2_dealt = keep.tile([P, PASSES, PACK, 2 * P], U8, name="w2_dealt", align_bytes=64)
         w3_dealt = keep.tile([P, PASSES, PACK, P], I32, name="w3_dealt", align_bytes=64)
         hum_sb = [keep.tile([P, BANK], F32, name="hum_%d" % u, tag="unit_%d" % u) for u in range(UNITS)]
-        wgs_sb = [keep.tile([P, S], F32, name="wgs_%d" % t, tag="wgs_%d" % t) for t in range(PACK)]
+        wgs_sb = [keep.tile([P, S], F32, name="wgs_%d" % t, tag="wgs_%d" % t, align_bytes=64) for t in range(PACK)]
         page = [keep.tile([P, T2], F32, name="page_%d" % t) for t in range(PACK)]
         base_sb = keep.tile([P, PACK], F32, name="base_sb")
         w4_raw = keep.tile([P, PACK, N], F32, name="w4_raw")
         w4_bf = keep.tile([P, N, PACK], BF16, name="w4_bf", align_bytes=64)
-        w4_codes = keep.tile([P, N], U32, name="w4_codes", align_bytes=64)
         w4_scales = keep.tile([P, N], U8, name="w4_scales", align_bytes=64)
 
         def load_wgs(t, cols):
@@ -80,7 +81,7 @@ def tile_list_arrester_varistor_page_kernel(
             picked_rows = head.tile([P, S], U8, name="picked_rows")
             w_rows = head.tile([P, 2, H], U8, name="w_rows")
             staged = head.tile([P, S + 2 * H], U8, name="staged")
-            w1_raw = [head.tile([P, PACK, H], F32, name="w1_raw_%d" % a) for a in range(PASSES)]
+            w1_raw = [[head.tile([P, PACK, H // 2], F32, name="w1_raw_%d_%d" % (a, i)) for i in range(2)] for a in range(PASSES)]
             w1_bf = [head.tile([P, PACK, P, PACK], BF16, name="w1_bf_%d" % a, align_bytes=64) for a in range(PASSES)]
             w2_raw = head.tile([P, PASSES, 2 * H], U8, name="w2_raw")
             w3_raw = head.tile([P, PASSES, H], I32, name="w3_raw")
@@ -98,12 +99,16 @@ def tile_list_arrester_varistor_page_kernel(
             def load_table(a):
                 nc.sync.dma_start(out=table[a][:], in_=tab_words[a].rearrange("p n i -> p (n i)").bitcast(I32))
 
-            for a in range(PASSES):
-                load_table(a)
-            for a in range(PASSES):
-                nc.sync.dma_start(out=w1_raw[a][:], in_=w1[512 * a:512 * a + 512, :].rearrange("(p j) c -> p j c", j=PACK))
-            load_hum(0)
+            load_table(0)
             nc.sync.dma_start(out=w2_raw[:].bitcast(I32), in_=w2_words.rearrange("a p c -> p a c").bitcast(I32))
+            load_table(1)
+            for a in range(PASSES):
+                for half in range(2):
+                    nc.sync.dma_start(
+                        out=w1_raw[a][half][:],
+                        in_=w1[512 * a:512 * a + 512, 256 * half:256 * half + 256].rearrange("(p j) c -> p j c", j=PACK),
+                    )
+            load_hum(0)
             nc.sync.dma_start(out=w3_raw[:], in_=w3_words.rearrange("a p c i -> p a (c i)").bitcast(I32))
             load_hum(1)
             load_wgs(0, slice(0, BANK))
@@ -115,11 +120,12 @@ def tile_list_arrester_varistor_page_kernel(
             nc.sync.dma_start(out=base_sb[:], in_=base.rearrange("(p t) -> p t", t=PACK))
             for t in range(1, PACK):
                 load_hum(2 * t + 1)
+                if t == 1:
+                    nc.sync.dma_start(out=w4_raw[:], in_=w4.rearrange("(p j) n -> p j n", j=PACK))
                 load_wgs(t, slice(0, S))
                 nc.sync.dma_start(out=page[t][:], in_=page_in[t])
                 if t + 1 < PACK:
                     load_hum(2 * t + 2)
-            nc.sync.dma_start(out=w4_raw[:], in_=w4.rearrange("(p j) n -> p j n", j=PACK))
 
             nc.vector.tensor_copy(picked_rows[:], tab_rows[:].indirect(idx1[:]))
             nc.vector.tensor_copy(staged[:, 0:S].bitcast(I32), picked_rows[:].bitcast(I32))
@@ -141,22 +147,29 @@ def tile_list_arrester_varistor_page_kernel(
                     table[a][:].bitcast(U32).indirect(idx1[:, LIST_COLS * h:LIST_COLS * (h + 1)]),
                 )
 
-            for a in range(PASSES):
-                for h in range(HALVES):
-                    pick(a, h)
-            for a in range(PASSES):
-                dealt = w1_bf[a][:].rearrange("p t m j -> p m t j")
-                raw = w1_raw[a][:].rearrange("p j (m t) -> p m t j", t=PACK)
-                nc.vector.tensor_copy(dealt[:, :W1_SPLIT], raw[:, :W1_SPLIT])
-                nc.scalar.copy(dealt[:, W1_SPLIT:], raw[:, W1_SPLIT:])
-                nc.vector.quantize_mx(
-                    out=w1_codes[a][:].bitcast(FP8X4), scales=w1_scales[a][:],
-                    in_=w1_bf[a][:].rearrange("p t m j -> p (t m j)"),
-                )
+            for h in range(HALVES):
+                pick(0, h)
             nc.vector.tensor_copy(
                 w2_dealt[:].rearrange("p a t (m e) -> p a t m e", e=2),
                 w2_raw[:].rearrange("p a (m t e) -> p a t m e", t=PACK, e=2),
             )
+            for h in range(HALVES):
+                pick(1, h)
+            for a in range(PASSES):
+                dealt = w1_bf[a][:].rearrange("p t m j -> p m t j")
+                for half in range(2):
+                    raw = w1_raw[a][half][:].rearrange("p j (m t) -> p m t j", t=PACK)
+                    split = W1_SPLIT[a][half]
+                    if split > 0:
+                        nc.vector.tensor_copy(dealt[:, 64 * half:64 * half + split], raw[:, :split])
+                    if split < 64:
+                        nc.scalar.copy(dealt[:, 64 * half + split:64 * half + 64], raw[:, split:])
+                flat = w1_bf[a][:].rearrange("p t m j -> p (t m j)")
+                for lo, hi in ((0, 1), (1, 2), (2, 4)) if a == 1 else ((0, 4),):
+                    nc.vector.quantize_mx(
+                        out=w1_codes[a][:, P * lo:P * hi].bitcast(FP8X4), scales=w1_scales[a][:, P * lo:P * hi],
+                        in_=flat[:, BANK * lo:BANK * hi],
+                    )
             nc.vector.tensor_copy(
                 w3_dealt[:].rearrange("p a t m -> p a m t"),
                 w3_raw[:].rearrange("p a (m t) -> p a m t", t=PACK),
@@ -164,11 +177,14 @@ def tile_list_arrester_varistor_page_kernel(
 
         tail = ctx.enter_context(tc.tile_pool(name="tail", bufs=1))
         page_pairs = [tail.tile([P, 2, BANK, 2], BF16, name="page_pairs_%d" % c) for c in range(CHUNKS)]
-        x_pairs = [tail.tile([P, 2, BANK, 2], BF16, name="x_pairs_%d" % h) for h in range(HALVES)]
+        x_pairs = [tail.tile([P, 2, BANK, 2], BF16, name="x_pairs_%d" % h, tag="x_pairs_%d" % h, align_bytes=64) for h in range(HALVES)]
         page_codes = tail.tile([P, T2], I32, name="page_codes", align_bytes=64)
         page_scales = tail.tile([P, T2], U8, name="page_scales", align_bytes=64)
 
-        read = [[tail.tile([P, BANK], F32, name="read_%d_%d" % (t, h)) for h in range(HALVES)] for t in range(PACK)]
+        after, read = {}, {}
+        pre_of = {}
+        floored = {}
+        floored_last = tail.tile([P, HALVES, BANK], F32, name="floored_last", tag="read_last", align_bytes=64)
         sums, tanh_of, third, prod = {}, {}, {}, {}
 
         def products(u):
@@ -196,81 +212,118 @@ def tile_list_arrester_varistor_page_kernel(
             t, h = divmod(u, HALVES)
             cols = slice(BANK * h, BANK * (h + 1))
             pre = ring.tile([P, BANK], F32, name="pre")
-            if u == 0:
+            if t == 0:
                 nc.vector.tensor_tensor(pre[:], sums[u][0][:], hum_sb[u][:], ALU.add)
             else:
                 nc.scalar.copy(pre[:], sums[u][0][:])
                 nc.gpsimd.tensor_tensor(pre[:], pre[:], hum_sb[u][:], ALU.add)
+            if u > 0:
                 third[u] = ring.tile([P, BANK], F32, name="third")
                 nc.scalar.copy(third[u][:], sums[u][2][:])
-            tanh_of[u] = ring.tile([P, BANK], F32, name="tanh_of")
+            pre_of[u] = pre
+
+        def activate(u):
+            t, h = divmod(u, HALVES)
+            pre = pre_of[u]
+            if h == 1:
+                tanh_of[u] = keep.tile([P, BANK], F32, name="tanh_odd_%d" % t, tag="after_%d" % t)
+            else:
+                tanh_of[u] = ring.tile([P, BANK], F32, name="tanh_even", bufs=2)
             nc.scalar.activation(tanh_of[u][:], pre[:], ACT.Tanh)
             prod[u] = ring.tile([P, BANK], F32, name="prod")
             nc.vector.tensor_tensor(prod[u][:], sums[u][1][:], tanh_of[u][:], ALU.mult)
+            if h == 1:
+                after[t] = keep.tile([P, 1 + HALVES, BANK], F32, name="after_%d" % t, tag="after_%d" % t)
+                read[t - 1] = [after[t][:, 1 + i, :] for i in range(HALVES)]
 
         def back(u):
             t, h = divmod(u, HALVES)
             cols = slice(BANK * h, BANK * (h + 1))
-            slot = "unit_%d" % (u + 1) if 0 < u < UNITS - 1 else "cells_%d" % u
-            cells = keep.tile([P, BANK], F32, name="cells_%d" % u, tag=slot)
+            if h == 0:
+                cells = after[t][:, 0, :]
+            else:
+                cells = ring.tile([P, BANK], F32, name="cells", bufs=2)[:]
             if u == 0:
                 nc.vector.tensor_tensor(prod[u][:], prod[u][:], sums[u][2][:], ALU.subtract)
-                nc.vector.tensor_tensor(cells[:], prod[u][:], wgs_sb[t][:, cols], ALU.mult)
+                nc.vector.tensor_tensor(cells, prod[u][:], wgs_sb[t][:, cols], ALU.mult)
             else:
                 nc.gpsimd.tensor_tensor(prod[u][:], prod[u][:], third[u][:], ALU.subtract)
-                nc.gpsimd.tensor_tensor(cells[:], prod[u][:], wgs_sb[t][:, cols], ALU.mult)
-            nc.vector.tensor_copy(page[t][:].indirect(idx2[:, LIST_COLS * h:LIST_COLS * (h + 1)]), cells[:])
+                nc.gpsimd.tensor_tensor(cells, prod[u][:], wgs_sb[t][:, cols], ALU.mult)
+            nc.vector.tensor_copy(page[t][:].indirect(idx2[:, LIST_COLS * h:LIST_COLS * (h + 1)]), cells)
 
         def read_page(t):
             nc.sync.dma_start(out=page_out[t], in_=page[t][:])
             for h in range(HALVES):
-                nc.vector.tensor_copy(read[t][h][:], page[t][:].indirect(idx3[:, LIST_COLS * h:LIST_COLS * (h + 1)]))
+                nc.vector.tensor_copy(read[t][h], page[t][:].indirect(idx3[:, LIST_COLS * h:LIST_COLS * (h + 1)]))
 
         def floor_at_base(t, h):
-            nc.vector.tensor_scalar(x_pairs[h][:, t // 2, :, t % 2], read[t][h][:], late_base[:, t:t + 1], None, ALU.max)
+            if t < PACK - 2:
+                floored[t, h] = keep.tile([P, BANK], F32, name="floored_%d_%d" % (t, h), tag="unit_%d" % (2 * t + 4 + h))[:]
+            else:
+                floored[t, h] = floored_last[:, h, :]
+            nc.gpsimd.tensor_scalar(floored[t, h], read[t][h], F32_MAX, base_sb[:, t:t + 1], ALU.min, ALU.max)
+
+        def round_x(t):
+            for h in range(HALVES):
+                nc.scalar.copy(x_pairs[h][:, t // 2, :, t % 2], floored[t, h])
 
         def round_page(t):
             for c in range(CHUNKS):
                 nc.scalar.copy(page_pairs[c][:, t // 2, :, t % 2], page[t][:, BANK * c:BANK * (c + 1)])
 
-        def weave(pairs):
-            woven = ring.tile([P, BANK * PACK], BF16, name="woven", align_bytes=64, bufs=2)
+        def weave(pairs, slot):
+            woven = tail.tile([P, BANK * PACK], BF16, name="woven", tag=slot, align_bytes=64, bufs=2 if slot == "woven" else 1)
             nc.vector.tensor_copy(
                 woven[:].bitcast(I32).rearrange("p (j u) -> p j u", u=2),
                 pairs[:].rearrange("p u j e -> p u (j e)").bitcast(I32).rearrange("p u j -> p j u"),
             )
             return woven
 
-        products(0)
-        front(0)
-        for u in range(UNITS):
-            if u + 1 < UNITS:
-                products(u + 1)
-                front(u + 1)
-            back(u)
-            if u % HALVES == HALVES - 1:
-                read_page(u // HALVES)
-            if u % HALVES == 0 and u > 0:
-                round_page(u // HALVES - 1)
-
-        nc.scalar.activation(warm[:, 1:2], tanh_of[UNITS - 1][:, 0:1], ACT.Sqrt, bias=1.0, scale=0.0)
-        nc.scalar.copy(w4_bf[:], w4_raw[:].rearrange("p j n -> p n j"))
+        for u in range(HALVES):
+            products(u)
+            front(u)
+            activate(u)
+        for t in range(PACK):
+            units = range(HALVES * t, HALVES * (t + 1))
+            ahead = range(HALVES * (t + 1), min(HALVES * (t + 2), UNITS))
+            if t > 0:
+                read_page(t - 1)
+            for u in units:
+                back(u)
+            for u in ahead:
+                products(u)
+                front(u)
+            if t > 0:
+                for h in range(HALVES):
+                    floor_at_base(t - 1, h)
+                round_page(t - 1)
+            if t == 0:
+                nc.scalar.copy(w4_bf[:], w4_raw[:].rearrange("p j n -> p n j"))
+            if t > 1:
+                round_x(t - 2)
+            for u in ahead:
+                activate(u)
+        round_x(PACK - 2)
+        nc.scalar.activation(warm[:, 1:2], floored[PACK - 2, 1][:, 0:1], ACT.Sqrt, bias=1.0, scale=0.0)
+        w4_codes = keep.tile([P, N], U32, name="w4_codes", tag="wgs_%d" % (PACK - 1), align_bytes=64)
         for lo, hi in ((0, 256), (256, N)):
             nc.vector.quantize_mx(
                 out=w4_codes[:, lo:hi].bitcast(FP8X4), scales=w4_scales[:, lo:hi],
                 in_=w4_bf[:, lo:hi, :].rearrange("p n j -> p (n j)"),
             )
+        nc.sync.dma_start(out=page_out[PACK - 1], in_=page[PACK - 1][:])
         round_page(PACK - 1)
-        late_base = keep.tile([P, PACK], F32, name="late_base", tag="wgs_%d" % (PACK - 1))
-        nc.gpsimd.tensor_copy(late_base[:], base_sb[:])
 
         for h in range(HALVES):
-            for t in range(PACK):
-                floor_at_base(t, h)
-            woven = weave(x_pairs[h])
+            last = tail.tile([P, BANK], F32, name="read_last_%d" % h, tag="x_first" if h else "read_last", align_bytes=64)
+            nc.vector.tensor_copy(last[:], page[PACK - 1][:].indirect(idx3[:, LIST_COLS * h:LIST_COLS * (h + 1)]))
+            nc.vector.tensor_scalar(x_pairs[h][:, 1, :, 1], last[:], base_sb[:, PACK - 1:PACK], None, ALU.max)
+            woven = weave(x_pairs[h], "woven" if h else "x_first")
             x_codes = ring.tile([P, BANK], U32, name="x_codes", align_bytes=64, bufs=2)
             x_scales = ring.tile([P, BANK], U8, name="x_scales", align_bytes=64, bufs=2)
             nc.vector.quantize_mx(out=x_codes[:].bitcast(FP8X4), scales=x_scales[:], in_=woven[:])
+            size = tail.tile([P, N // P, BANK], F32, name="size_%d" % h)
+            root = tail.tile([P, N // P, BANK], F32, name="root_%d" % h)
             for n in range(N // P):
                 cols = slice(P * n, P * (n + 1))
                 score = psum.tile([P, BANK], F32, name="bank_%d" % n)
@@ -278,18 +331,19 @@ def tile_list_arrester_varistor_page_kernel(
                     out=score[:], lhsT=w4_codes[:, cols].bitcast(FP8X4), lhsT_scale=w4_scales[:, cols],
                     rhs=x_codes[:].bitcast(FP8X4), rhs_scale=x_scales[:], start=True, stop=True,
                 )
-                size = ring.tile([P, BANK], F32, name="pre")
-                nc.scalar.activation(size[:], score[:], ACT.Abs)
-                root = tail.tile([P, BANK], F32, name="root_%d_%d" % (h, n))
-                nc.scalar.activation(root[:], size[:], ACT.Sqrt, bias=1.0)
-                nc.sync.dma_start(out=out_0[cols, BANK * h:BANK * (h + 1)], in_=root[:])
+                nc.scalar.activation(size[:, n, :], score[:], ACT.Abs)
+            for lo, hi in ((0, 2), (2, 3)) if h else ((0, 3),):
+                nc.scalar.activation(root[:, lo:hi, :], size[:, lo:hi, :], ACT.Sqrt, bias=1.0)
+                nc.scalar.dma_start(out=scores_out[:, lo:hi, BANK * h:BANK * (h + 1)], in_=root[:, lo:hi, :])
 
         words_out = out_2[0].rearrange("p m i -> p (m i)").bitcast(I32)
         for c in range(CHUNKS):
             cols = slice(BANK * c, BANK * (c + 1))
-            woven = weave(page_pairs[c])
+            woven = weave(page_pairs[c], "woven" if c else "x_pairs_0")
             nc.vector.quantize_mx(out=page_codes[:, cols].bitcast(FP8X4), scales=page_scales[:, cols], in_=woven[:])
-            nc.sync.dma_start(out=words_out[:, cols], in_=page_codes[:, cols])
+            if c % 2 == 1:
+                both = slice(BANK * (c - 1), BANK * (c + 1))
+                nc.sync.dma_start(out=words_out[:, both], in_=page_codes[:, both])
         for quad in range(4):
             nc.sync.dma_start(
                 out=out_3[0, 4 * quad:4 * quad + 4, :].bitcast(I32),

@@ -54,10 +54,10 @@ def tile_list_arrester_varistor_page_kernel(
         w1_codes = [keep.tile([P, H], U32, name="w1_codes_%d" % a, align_bytes=64) for a in range(PASSES)]
         w1_scales = [keep.tile([P, H], U8, name="w1_scales_%d" % a, align_bytes=64) for a in range(PASSES)]
         w2_dealt = keep.tile([P, PASSES, PACK, 2 * P], U8, name="w2_dealt", align_bytes=64)
-        w3_dealt = keep.tile([P, PASSES, PACK, P], I32, name="w3_dealt", align_bytes=64)
-        hum_sb = [keep.tile([P, BANK], F32, name="hum_%d" % u, tag="unit_%d" % u) for u in range(UNITS)]
+        hum_sb = [keep.tile([P, BANK], F32, name="hum_%d" % u, tag="unit_%d" % u, align_bytes=64) for u in range(UNITS)]
         wgs_sb = [keep.tile([P, S], F32, name="wgs_%d" % t, tag="wgs_%d" % t, align_bytes=64) for t in range(PACK)]
         page = [keep.tile([P, T2], F32, name="page_%d" % t) for t in range(PACK)]
+        w3_raw = keep.tile([P, PASSES, H], I32, name="w3_raw")
         base_sb = keep.tile([P, PACK], F32, name="base_sb")
         w4_raw = keep.tile([P, PACK, N], F32, name="w4_raw")
         w4_bf = keep.tile([P, N, PACK], BF16, name="w4_bf", align_bytes=64)
@@ -84,7 +84,6 @@ def tile_list_arrester_varistor_page_kernel(
             w1_raw = [[head.tile([P, PACK, H // 2], F32, name="w1_raw_%d_%d" % (a, i)) for i in range(2)] for a in range(PASSES)]
             w1_bf = [head.tile([P, PACK, P, PACK], BF16, name="w1_bf_%d" % a, align_bytes=64) for a in range(PASSES)]
             w2_raw = head.tile([P, PASSES, 2 * H], U8, name="w2_raw")
-            w3_raw = head.tile([P, PASSES, H], I32, name="w3_raw")
 
             for lo, hi in ((32, 64), (64, 128)):
                 nc.vector.memset(tab_rows[lo:hi, :].bitcast(I32), 0)
@@ -112,20 +111,19 @@ def tile_list_arrester_varistor_page_kernel(
             nc.sync.dma_start(out=w3_raw[:], in_=w3_words.rearrange("a p c i -> p a (c i)").bitcast(I32))
             load_hum(1)
             load_wgs(0, slice(0, BANK))
-            nc.sync.dma_start(idx2[:], offs2)
             nc.sync.dma_start(out=page[0][:], in_=page_in[0])
-            load_hum(2)
             load_wgs(0, slice(BANK, S))
+            nc.sync.dma_start(idx2[:], offs2)
+            load_hum(2)
+            load_hum(3)
             nc.sync.dma_start(idx3[:], offs3)
+            nc.sync.dma_start(out=w4_raw[:], in_=w4.rearrange("(p j) n -> p j n", j=PACK))
             nc.sync.dma_start(out=base_sb[:], in_=base.rearrange("(p t) -> p t", t=PACK))
             for t in range(1, PACK):
-                load_hum(2 * t + 1)
-                if t == 1:
-                    nc.sync.dma_start(out=w4_raw[:], in_=w4.rearrange("(p j) n -> p j n", j=PACK))
+                for u in range(2 * t + 2, min(2 * t + 4, UNITS)):
+                    load_hum(u)
                 load_wgs(t, slice(0, S))
                 nc.sync.dma_start(out=page[t][:], in_=page_in[t])
-                if t + 1 < PACK:
-                    load_hum(2 * t + 2)
 
             nc.vector.tensor_copy(picked_rows[:], tab_rows[:].indirect(idx1[:]))
             nc.vector.tensor_copy(staged[:, 0:S].bitcast(I32), picked_rows[:].bitcast(I32))
@@ -170,28 +168,28 @@ def tile_list_arrester_varistor_page_kernel(
                         out=w1_codes[a][:, P * lo:P * hi].bitcast(FP8X4), scales=w1_scales[a][:, P * lo:P * hi],
                         in_=flat[:, BANK * lo:BANK * hi],
                     )
-            nc.vector.tensor_copy(
-                w3_dealt[:].rearrange("p a t m -> p a m t"),
-                w3_raw[:].rearrange("p a (m t) -> p a m t", t=PACK),
-            )
 
         tail = ctx.enter_context(tc.tile_pool(name="tail", bufs=1))
-        page_pairs = [tail.tile([P, 2, BANK, 2], BF16, name="page_pairs_%d" % c) for c in range(CHUNKS)]
         x_pairs = [tail.tile([P, 2, BANK, 2], BF16, name="x_pairs_%d" % h, tag="x_pairs_%d" % h, align_bytes=64) for h in range(HALVES)]
         page_codes = tail.tile([P, T2], I32, name="page_codes", align_bytes=64)
         page_scales = tail.tile([P, T2], U8, name="page_scales", align_bytes=64)
 
         after, read = {}, {}
-        pre_of = {}
+        summed, cells_of = {}, {}
         floored = {}
-        floored_last = tail.tile([P, HALVES, BANK], F32, name="floored_last", tag="read_last", align_bytes=64)
         sums, tanh_of, third, prod = {}, {}, {}, {}
 
-        def products(u):
+        def first_product(u):
+            sums[u] = []
+            products(u, (0,))
+
+        def other_products(u):
+            products(u, (1, 2))
+
+        def products(u, which):
             t, h = divmod(u, HALVES)
             cols = slice(P * t, P * (t + 1))
-            banks = []
-            for w in range(3):
+            for w in which:
                 bank = psum.tile([P, BANK], F32, name="bank_%d" % w)
                 for a in range(PASSES):
                     if w == 0:
@@ -205,74 +203,95 @@ def tile_list_arrester_varistor_page_kernel(
                         rhs=picked[a][h][:].bitcast(FP8X4), rhs_scale=planes[:, a, BANK * h:BANK * (h + 1)],
                         start=(a == 0), stop=(a == PASSES - 1),
                     )
-                banks.append(bank)
-            sums[u] = banks
+                sums[u].append(bank)
 
-        def front(u):
+        def work(name, slot, rows=1):
+            return keep.tile([P, rows, BANK], F32, name=name, tag=slot, align_bytes=64)
+
+        def diff_slot(t):
+            return "cells_%d" % (t - 1)
+
+        def even_slot(t):
+            return ("", "unit_5", "after_1", "summed_1")[t]
+
+        def copy_third(u):
+            third[u] = ring.tile([P, BANK], F32, name="third")
+            nc.scalar.copy(third[u][:], sums[u][2][:])
+
+        def add_hum(u):
+            if u < HALVES:
+                slot = "summed_%d" % u
+            elif u == 2:
+                slot = diff_slot(0)
+            elif u == 6:
+                slot = even_slot(1)
+            else:
+                slot = "unit_%d" % (u - 1)
+            summed[u] = work("summed_%d" % u, slot)[:, 0, :]
+            if u < HALVES:
+                nc.vector.tensor_tensor(summed[u], sums[u][0][:], hum_sb[u][:], ALU.add)
+            else:
+                first = ring.tile([P, BANK], F32, name="first", bufs=3)
+                nc.scalar.copy(first[:], sums[u][0][:])
+                nc.gpsimd.tensor_tensor(summed[u], first[:], hum_sb[u][:], ALU.add)
+
+        def tanh(u):
+            t, h = divmod(u, HALVES)
+            tanh_of[u] = work("tanh_%d" % u, ("after_%d" if h else "tanh_even_%d") % t)[:, 0, :]
+            nc.scalar.activation(tanh_of[u], summed[u], ACT.Tanh)
+
+        def multiply(u):
+            t, h = divmod(u, HALVES)
+            slot = "tanh_even_%d" % t if h and t else diff_slot(t)
+            if t == PACK - 1:
+                slot = diff_slot(t) if h else "after_%d" % (t - 1)
+            prod[u] = work("prod_%d" % u, slot)[:, 0, :]
+            if u != UNITS - 2:
+                nc.vector.tensor_tensor(prod[u], sums[u][1][:], tanh_of[u], ALU.mult)
+            else:
+                second = ring.tile([P, BANK], F32, name="first", bufs=3)
+                nc.scalar.copy(second[:], sums[u][1][:])
+                nc.gpsimd.tensor_tensor(prod[u], second[:], tanh_of[u], ALU.mult)
+            if h == 1 and t > 0:
+                after[t] = work("after_%d" % t, "after_%d" % t, 1 + HALVES)
+                read[t - 1] = after[t][:, 1:, :].rearrange("p h j -> p (h j)")
+
+        def combine(u):
             t, h = divmod(u, HALVES)
             cols = slice(BANK * h, BANK * (h + 1))
-            pre = ring.tile([P, BANK], F32, name="pre")
+            cells = work("cells_%d" % u, "cells_%d" % t if h else "summed_0")[:, 0, :] if h or t == 0 else after[t][:, 0, :]
             if t == 0:
-                nc.vector.tensor_tensor(pre[:], sums[u][0][:], hum_sb[u][:], ALU.add)
+                diff = prod[u] if h else work("diff_0", "tanh_even_0")[:, 0, :]
+                nc.vector.tensor_tensor(diff, prod[u], sums[u][2][:], ALU.subtract)
             else:
-                nc.scalar.copy(pre[:], sums[u][0][:])
-                nc.gpsimd.tensor_tensor(pre[:], pre[:], hum_sb[u][:], ALU.add)
-            if u > 0:
-                third[u] = ring.tile([P, BANK], F32, name="third")
-                nc.scalar.copy(third[u][:], sums[u][2][:])
-            pre_of[u] = pre
+                diff = work("diff_%d" % u, even_slot(t))[:, 0, :]
+                nc.gpsimd.tensor_tensor(diff, prod[u], third[u][:], ALU.subtract)
+            nc.gpsimd.tensor_tensor(cells, diff, wgs_sb[t][:, cols], ALU.mult)
+            cells_of[u] = cells
 
-        def activate(u):
+        def put(u):
             t, h = divmod(u, HALVES)
-            pre = pre_of[u]
-            if h == 1:
-                tanh_of[u] = keep.tile([P, BANK], F32, name="tanh_odd_%d" % t, tag="after_%d" % t)
-            else:
-                tanh_of[u] = ring.tile([P, BANK], F32, name="tanh_even", bufs=2)
-            nc.scalar.activation(tanh_of[u][:], pre[:], ACT.Tanh)
-            prod[u] = ring.tile([P, BANK], F32, name="prod")
-            nc.vector.tensor_tensor(prod[u][:], sums[u][1][:], tanh_of[u][:], ALU.mult)
-            if h == 1:
-                after[t] = keep.tile([P, 1 + HALVES, BANK], F32, name="after_%d" % t, tag="after_%d" % t)
-                read[t - 1] = [after[t][:, 1 + i, :] for i in range(HALVES)]
-
-        def back(u):
-            t, h = divmod(u, HALVES)
-            cols = slice(BANK * h, BANK * (h + 1))
-            if h == 0:
-                cells = after[t][:, 0, :]
-            else:
-                cells = ring.tile([P, BANK], F32, name="cells", bufs=2)[:]
-            if u == 0:
-                nc.vector.tensor_tensor(prod[u][:], prod[u][:], sums[u][2][:], ALU.subtract)
-                nc.vector.tensor_tensor(cells, prod[u][:], wgs_sb[t][:, cols], ALU.mult)
-            else:
-                nc.gpsimd.tensor_tensor(prod[u][:], prod[u][:], third[u][:], ALU.subtract)
-                nc.gpsimd.tensor_tensor(cells, prod[u][:], wgs_sb[t][:, cols], ALU.mult)
-            nc.vector.tensor_copy(page[t][:].indirect(idx2[:, LIST_COLS * h:LIST_COLS * (h + 1)]), cells)
+            nc.vector.tensor_copy(page[t][:].indirect(idx2[:, LIST_COLS * h:LIST_COLS * (h + 1)]), cells_of[u])
 
         def read_page(t):
             nc.sync.dma_start(out=page_out[t], in_=page[t][:])
-            for h in range(HALVES):
-                nc.vector.tensor_copy(read[t][h], page[t][:].indirect(idx3[:, LIST_COLS * h:LIST_COLS * (h + 1)]))
+            nc.vector.tensor_copy(read[t], page[t][:].indirect(idx3[:]))
 
-        def floor_at_base(t, h):
-            if t < PACK - 2:
-                floored[t, h] = keep.tile([P, BANK], F32, name="floored_%d_%d" % (t, h), tag="unit_%d" % (2 * t + 4 + h))[:]
-            else:
-                floored[t, h] = floored_last[:, h, :]
-            nc.gpsimd.tensor_scalar(floored[t, h], read[t][h], F32_MAX, base_sb[:, t:t + 1], ALU.min, ALU.max)
+        def floor_at_base(t):
+            floored[t] = work("floored_%d" % t, even_slot(t + 1) if t else "unit_%d" % (UNITS - 1), HALVES)
+            if True:
+                nc.gpsimd.tensor_scalar(floored[t][:].rearrange("p h j -> p (h j)"), read[t], F32_MAX, base_sb[:, t:t + 1], ALU.min, ALU.max)
 
         def round_x(t):
             for h in range(HALVES):
-                nc.scalar.copy(x_pairs[h][:, t // 2, :, t % 2], floored[t, h])
+                nc.scalar.copy(x_pairs[h][:, t // 2, :, t % 2], floored[t][:, h, :])
 
         def round_page(t):
             for c in range(CHUNKS):
                 nc.scalar.copy(page_pairs[c][:, t // 2, :, t % 2], page[t][:, BANK * c:BANK * (c + 1)])
 
         def weave(pairs, slot):
-            woven = tail.tile([P, BANK * PACK], BF16, name="woven", tag=slot, align_bytes=64, bufs=2 if slot == "woven" else 1)
+            woven = tail.tile([P, BANK * PACK], BF16, name="woven", tag=slot, align_bytes=64)
             nc.vector.tensor_copy(
                 woven[:].bitcast(I32).rearrange("p (j u) -> p j u", u=2),
                 pairs[:].rearrange("p u j e -> p u (j e)").bitcast(I32).rearrange("p u j -> p j u"),
@@ -280,32 +299,52 @@ def tile_list_arrester_varistor_page_kernel(
             return woven
 
         for u in range(HALVES):
-            products(u)
-            front(u)
-            activate(u)
+            first_product(u)
+            add_hum(u)
+            tanh(u)
+        w3_dealt = keep.tile([P, PASSES, PACK, P], I32, name="w3_dealt", tag="unit_0", align_bytes=64)
+        nc.vector.tensor_copy(
+            w3_dealt[:].rearrange("p a t m -> p a m t"),
+            w3_raw[:].rearrange("p a (m t) -> p a m t", t=PACK),
+        )
+        for u in range(HALVES):
+            other_products(u)
+        page_pairs = []
         for t in range(PACK):
             units = range(HALVES * t, HALVES * (t + 1))
-            ahead = range(HALVES * (t + 1), min(HALVES * (t + 2), UNITS))
-            if t > 0:
+            if t == 0:
+                for u in units:
+                    multiply(u)
+                    combine(u)
+            else:
+                for u in units:
+                    multiply(u)
                 read_page(t - 1)
+                for u in units:
+                    combine(u)
             for u in units:
-                back(u)
-            for u in ahead:
-                products(u)
-                front(u)
+                put(u)
+            for u in range(HALVES * (t + 2) if t else HALVES, min(HALVES * (t + 3), UNITS)):
+                first_product(u)
+                add_hum(u)
+                tanh(u)
+            for u in range(HALVES * (t + 1), min(HALVES * (t + 2), UNITS)):
+                other_products(u)
+                copy_third(u)
+            if t == 1:
+                for c, slot in enumerate(("unit_2", "unit_3", "unit_4", "cells_0")):
+                    page_pairs.append(keep.tile([P, 2, BANK, 2], BF16, name="page_pairs_%d" % c, tag=slot, align_bytes=64))
             if t > 0:
-                for h in range(HALVES):
-                    floor_at_base(t - 1, h)
+                floor_at_base(t - 1)
                 round_page(t - 1)
             if t == 0:
                 nc.scalar.copy(w4_bf[:], w4_raw[:].rearrange("p j n -> p n j"))
             if t > 1:
                 round_x(t - 2)
-            for u in ahead:
-                activate(u)
+            if t == PACK - 1:
+                nc.scalar.activation(warm[:, 1:2], third[UNITS - 1][:, 0:1], ACT.Sqrt, bias=1.0, scale=0.0)
         round_x(PACK - 2)
-        nc.scalar.activation(warm[:, 1:2], floored[PACK - 2, 1][:, 0:1], ACT.Sqrt, bias=1.0, scale=0.0)
-        w4_codes = keep.tile([P, N], U32, name="w4_codes", tag="wgs_%d" % (PACK - 1), align_bytes=64)
+        w4_codes = keep.tile([P, N], U32, name="w4_codes", tag="cells_%d" % (PACK - 1), align_bytes=64)
         for lo, hi in ((0, 256), (256, N)):
             nc.vector.quantize_mx(
                 out=w4_codes[:, lo:hi].bitcast(FP8X4), scales=w4_scales[:, lo:hi],
@@ -315,15 +354,18 @@ def tile_list_arrester_varistor_page_kernel(
         round_page(PACK - 1)
 
         for h in range(HALVES):
-            last = tail.tile([P, BANK], F32, name="read_last_%d" % h, tag="x_first" if h else "read_last", align_bytes=64)
-            nc.vector.tensor_copy(last[:], page[PACK - 1][:].indirect(idx3[:, LIST_COLS * h:LIST_COLS * (h + 1)]))
-            nc.vector.tensor_scalar(x_pairs[h][:, 1, :, 1], last[:], base_sb[:, PACK - 1:PACK], None, ALU.max)
+            if h == 0:
+                last = work("read_last_0", even_slot(PACK - 1))[:, 0, :]
+            else:
+                last = tail.tile([P, BANK], F32, name="read_last_1", tag="x_pairs_0", align_bytes=64)[:]
+            nc.vector.tensor_copy(last, page[PACK - 1][:].indirect(idx3[:, LIST_COLS * h:LIST_COLS * (h + 1)]))
+            nc.vector.tensor_scalar(x_pairs[h][:, 1, :, 1], last, base_sb[:, PACK - 1:PACK], None, ALU.max)
             woven = weave(x_pairs[h], "woven" if h else "x_first")
-            x_codes = ring.tile([P, BANK], U32, name="x_codes", align_bytes=64, bufs=2)
-            x_scales = ring.tile([P, BANK], U8, name="x_scales", align_bytes=64, bufs=2)
+            x_codes = tail.tile([P, BANK], U32, name="x_codes_%d" % h, align_bytes=64)
+            x_scales = tail.tile([P, BANK], U8, name="x_scales_%d" % h, align_bytes=64)
             nc.vector.quantize_mx(out=x_codes[:].bitcast(FP8X4), scales=x_scales[:], in_=woven[:])
-            size = tail.tile([P, N // P, BANK], F32, name="size_%d" % h)
-            root = tail.tile([P, N // P, BANK], F32, name="root_%d" % h)
+            size = work("size_%d" % h, "after_%d" % h, N // P)
+            root = work("root_%d" % h, "after_%d" % (3 - h), N // P)
             for n in range(N // P):
                 cols = slice(P * n, P * (n + 1))
                 score = psum.tile([P, BANK], F32, name="bank_%d" % n)
@@ -339,13 +381,13 @@ def tile_list_arrester_varistor_page_kernel(
         words_out = out_2[0].rearrange("p m i -> p (m i)").bitcast(I32)
         for c in range(CHUNKS):
             cols = slice(BANK * c, BANK * (c + 1))
-            woven = weave(page_pairs[c], "woven" if c else "x_pairs_0")
+            woven = weave(page_pairs[c], ("x_pairs_0", "x_first", "x_pairs_1", "woven")[c])
             nc.vector.quantize_mx(out=page_codes[:, cols].bitcast(FP8X4), scales=page_scales[:, cols], in_=woven[:])
-            if c % 2 == 1:
-                both = slice(BANK * (c - 1), BANK * (c + 1))
+            if c > 0:
+                both = slice(BANK * (c - 1), BANK * (c + 1)) if c == 1 else cols
                 nc.sync.dma_start(out=words_out[:, both], in_=page_codes[:, both])
         for quad in range(4):
-            nc.sync.dma_start(
+            (nc.gpsimd if quad % 2 else nc.sync).dma_start(
                 out=out_3[0, 4 * quad:4 * quad + 4, :].bitcast(I32),
                 in_=page_scales[32 * quad:32 * quad + 4, :].bitcast(I32),
             )

@@ -18,14 +18,18 @@ ACT = mybir.ActivationFunctionType
 
 P = 128
 PACK = 4
-PASSES = K // (P * PACK)
+PASS = P * PACK
+PASSES = K // PASS
+BLOCKS = PASS // 32
+QUADS = 4
 BANK = 512
 HALVES = S // BANK
-UNITS = PACK * HALVES
 CHUNKS = T2 // BANK
 LIST_COLS = BANK // 16
 F32_MAX = 3.4028234663852886e38
-W1_SPLIT = ((0, 40), (64, 42))
+BANK_BUFS = (4, 2, 2)
+W1_ON_VECTOR = (76, 84)
+QUAD_ORDER = (0, 2, 1, 3)
 
 
 def tile_list_arrester_varistor_page_kernel(
@@ -36,44 +40,55 @@ def tile_list_arrester_varistor_page_kernel(
     hum_rows = hum.rearrange("(p t) j -> t p j", t=PACK)
     wgs_rows = wgs.rearrange("(q t) j -> t q j", t=PACK)
     page_in = page0.rearrange("(p t) c -> t p c", t=PACK)
-    scores_out = out_0.rearrange("(n p) m -> p n m", p=P)
     page_out = out_1.rearrange("(p t) c -> t p c", t=PACK)
+    scores_out = out_0.rearrange("(n p) m -> p n m", p=P)
+    words_out = out_2[0].rearrange("p m i -> p (m i)").bitcast(I32)
+
+    def half(h):
+        return slice(BANK * h, BANK * (h + 1))
+
+    def entries(offsets, h):
+        return offsets[:, LIST_COLS * h:LIST_COLS * (h + 1)]
 
     with ExitStack() as ctx:
         lists = ctx.enter_context(tc.tile_pool(name="lists", bufs=1))
         keep = ctx.enter_context(tc.tile_pool(name="keep", bufs=1))
-        ring = ctx.enter_context(tc.tile_pool(name="ring", bufs=3))
         psum = ctx.enter_context(tc.psum_pool(name="psum", bufs=2))
+
+        def row_tile(name, tag):
+            return keep.tile([P, S], F32, name=name, tag=tag, align_bytes=64)
 
         idx1 = lists.tile([P, S // 16], U16, name="idx1")
         idx2 = lists.tile([P, S // 16], U16, name="idx2")
         idx3 = lists.tile([P, NREAD // 16], U16, name="idx3")
 
-        planes = keep.tile([P, PASSES, S + 2 * H], U8, name="planes", align_bytes=64)
-        picked = [[keep.tile([P, BANK], I32, name="picked_%d_%d" % (a, h), align_bytes=64) for h in range(HALVES)] for a in range(PASSES)]
+        given_scales = keep.tile([P, PASSES, S + 2 * H], U8, name="given_scales", align_bytes=64)
+        picked = [
+            [keep.tile([P, BANK], I32, name="picked_%d_%d" % (a, h), align_bytes=64) for h in range(HALVES)]
+            for a in range(PASSES)
+        ]
         w1_codes = [keep.tile([P, H], U32, name="w1_codes_%d" % a, align_bytes=64) for a in range(PASSES)]
         w1_scales = [keep.tile([P, H], U8, name="w1_scales_%d" % a, align_bytes=64) for a in range(PASSES)]
         w2_dealt = keep.tile([P, PASSES, PACK, 2 * P], U8, name="w2_dealt", align_bytes=64)
-        hum_sb = [keep.tile([P, BANK], F32, name="hum_%d" % u, tag="unit_%d" % u, align_bytes=64) for u in range(UNITS)]
-        wgs_sb = [keep.tile([P, S], F32, name="wgs_%d" % t, tag="wgs_%d" % t, align_bytes=64) for t in range(PACK)]
-        page = [keep.tile([P, T2], F32, name="page_%d" % t) for t in range(PACK)]
         w3_raw = keep.tile([P, PASSES, H], I32, name="w3_raw")
+        hum_first = [
+            keep.tile([P, BANK], F32, name="hum_0_%d" % h, tag="hum_0_%d" % h, align_bytes=64) for h in range(HALVES)
+        ]
+        hum_sb = {t: row_tile("hum_%d" % t, "hum_%d" % t) for t in range(1, PACK)}
+        wgs_sb = [row_tile("wgs_%d" % t, "wgs_%d" % t) for t in range(PACK)]
+        page = [keep.tile([P, T2], F32, name="page_%d" % t) for t in range(PACK)]
         base_sb = keep.tile([P, PACK], F32, name="base_sb")
         w4_raw = keep.tile([P, PACK, N], F32, name="w4_raw")
         w4_bf = keep.tile([P, N, PACK], BF16, name="w4_bf", align_bytes=64)
         w4_scales = keep.tile([P, N], U8, name="w4_scales", align_bytes=64)
 
-        def load_wgs(t, cols):
-            for quad in range(4):
-                nc.sync.dma_start(out=wgs_sb[t][32 * quad:32 * quad + 32, cols], in_=wgs_rows[t][:, cols])
-
-        def load_hum(u):
-            t, h = divmod(u, HALVES)
-            nc.sync.dma_start(out=hum_sb[u][:], in_=hum_rows[t][:, BANK * h:BANK * (h + 1)])
-
         warm = keep.tile([P, 2], F32, name="warm")
         nc.vector.memset(warm[:, 0:1], 0.0)
         nc.scalar.activation(warm[:, 1:2], warm[:, 0:1], ACT.Tanh)
+
+        def load_wgs(t):
+            for quad in QUAD_ORDER:
+                nc.sync.dma_start(out=wgs_sb[t][32 * quad:32 * quad + 32, :], in_=wgs_rows[t])
 
         with tc.tile_pool(name="head", bufs=1) as head:
             table = [head.tile([P, T], I32, name="table_%d" % a) for a in range(PASSES)]
@@ -81,48 +96,49 @@ def tile_list_arrester_varistor_page_kernel(
             picked_rows = head.tile([P, S], U8, name="picked_rows")
             w_rows = head.tile([P, 2, H], U8, name="w_rows")
             staged = head.tile([P, S + 2 * H], U8, name="staged")
-            w1_raw = [[head.tile([P, PACK, H // 2], F32, name="w1_raw_%d_%d" % (a, i)) for i in range(2)] for a in range(PASSES)]
-            w1_bf = [head.tile([P, PACK, P, PACK], BF16, name="w1_bf_%d" % a, align_bytes=64) for a in range(PASSES)]
+            w1_raw = [head.tile([P, PACK, H], F32, name="w1_raw_%d" % a) for a in range(PASSES)]
+            w1_bf = [
+                head.tile([P, PACK, P, PACK], BF16, name="w1_bf_%d" % a, align_bytes=64) for a in range(PASSES)
+            ]
             w2_raw = head.tile([P, PASSES, 2 * H], U8, name="w2_raw")
 
-            for lo, hi in ((32, 64), (64, 128)):
+            rows = PASSES * BLOCKS
+            for lo, hi in ((rows, 64), (64, P)):
                 nc.vector.memset(tab_rows[lo:hi, :].bitcast(I32), 0)
                 nc.vector.memset(w_rows[lo:hi].rearrange("p w c -> p (w c)").bitcast(I32), 0)
-            nc.vector.memset(planes[:].rearrange("p a c -> p (a c)").bitcast(I32), 0)
+            nc.vector.memset(given_scales[:].rearrange("p a c -> p (a c)").bitcast(I32), 0)
 
             nc.sync.dma_start(idx1[:], offs)
-            nc.sync.dma_start(out=tab_rows[0:32, :].bitcast(I32), in_=tab_scales.rearrange("a q n -> (a q) n").bitcast(I32))
+            nc.sync.dma_start(
+                out=tab_rows[0:rows, :].bitcast(I32), in_=tab_scales.rearrange("a q n -> (a q) n").bitcast(I32)
+            )
             for w, scales in enumerate((w2_scales, w3_scales)):
-                nc.sync.dma_start(out=w_rows[0:32, w, :].bitcast(I32), in_=scales.rearrange("a q c -> (a q) c").bitcast(I32))
-
-            def load_table(a):
-                nc.sync.dma_start(out=table[a][:], in_=tab_words[a].rearrange("p n i -> p (n i)").bitcast(I32))
-
-            load_table(0)
+                nc.sync.dma_start(
+                    out=w_rows[0:rows, w, :].bitcast(I32), in_=scales.rearrange("a q c -> (a q) c").bitcast(I32)
+                )
+            nc.sync.dma_start(out=table[0][:], in_=tab_words[0].rearrange("p n i -> p (n i)").bitcast(I32))
             nc.sync.dma_start(out=w2_raw[:].bitcast(I32), in_=w2_words.rearrange("a p c -> p a c").bitcast(I32))
-            load_table(1)
+            nc.sync.dma_start(out=table[1][:], in_=tab_words[1].rearrange("p n i -> p (n i)").bitcast(I32))
             for a in range(PASSES):
-                for half in range(2):
-                    nc.sync.dma_start(
-                        out=w1_raw[a][half][:],
-                        in_=w1[512 * a:512 * a + 512, 256 * half:256 * half + 256].rearrange("(p j) c -> p j c", j=PACK),
-                    )
-            load_hum(0)
+                nc.sync.dma_start(
+                    out=w1_raw[a][:], in_=w1[PASS * a:PASS * (a + 1), :].rearrange("(p j) c -> p j c", j=PACK)
+                )
+            nc.sync.dma_start(out=hum_first[0][:], in_=hum_rows[0][:, half(0)])
             nc.sync.dma_start(out=w3_raw[:], in_=w3_words.rearrange("a p c i -> p a (c i)").bitcast(I32))
-            load_hum(1)
-            load_wgs(0, slice(0, BANK))
+            nc.sync.dma_start(out=hum_first[1][:], in_=hum_rows[0][:, half(1)])
+            nc.sync.dma_start(out=hum_sb[1][:], in_=hum_rows[1])
+            nc.sync.dma_start(out=hum_sb[2][:], in_=hum_rows[2])
+            load_wgs(0)
             nc.sync.dma_start(out=page[0][:], in_=page_in[0])
-            load_wgs(0, slice(BANK, S))
             nc.sync.dma_start(idx2[:], offs2)
-            load_hum(2)
-            load_hum(3)
+            nc.sync.dma_start(out=hum_sb[3][:], in_=hum_rows[3])
             nc.sync.dma_start(idx3[:], offs3)
-            nc.sync.dma_start(out=w4_raw[:], in_=w4.rearrange("(p j) n -> p j n", j=PACK))
             nc.sync.dma_start(out=base_sb[:], in_=base.rearrange("(p t) -> p t", t=PACK))
-            for t in range(1, PACK):
-                for u in range(2 * t + 2, min(2 * t + 4, UNITS)):
-                    load_hum(u)
-                load_wgs(t, slice(0, S))
+            load_wgs(1)
+            nc.sync.dma_start(out=page[1][:], in_=page_in[1])
+            nc.sync.dma_start(out=w4_raw[:], in_=w4.rearrange("(p j) n -> p j n", j=PACK))
+            for t in range(2, PACK):
+                load_wgs(t)
                 nc.sync.dma_start(out=page[t][:], in_=page_in[t])
 
             nc.vector.tensor_copy(picked_rows[:], tab_rows[:].indirect(idx1[:]))
@@ -132,262 +148,200 @@ def tile_list_arrester_varistor_page_kernel(
                 w_rows[:].rearrange("p w (m t) -> p w t m", t=PACK),
             )
             for a in range(PASSES):
-                for quad in range(4):
-                    row = 16 * a + 4 * quad
-                    nc.gpsimd.dma_start(
-                        out=planes[32 * quad:32 * quad + 4, a, :].bitcast(I32),
+                for quad in range(QUADS):
+                    row = BLOCKS * a + 4 * quad
+                    (nc.scalar if a else nc.gpsimd).dma_start(
+                        out=given_scales[32 * quad:32 * quad + 4, a, :].bitcast(I32),
                         in_=staged[row:row + 4, :].bitcast(I32),
                     )
 
-            def pick(a, h):
-                nc.vector.tensor_copy(
-                    picked[a][h][:].bitcast(U32),
-                    table[a][:].bitcast(U32).indirect(idx1[:, LIST_COLS * h:LIST_COLS * (h + 1)]),
-                )
+            def pick(a):
+                for h in range(HALVES):
+                    nc.vector.tensor_copy(
+                        picked[a][h][:].bitcast(U32), table[a][:].bitcast(U32).indirect(entries(idx1, h))
+                    )
 
-            for h in range(HALVES):
-                pick(0, h)
+            pick(0)
             nc.vector.tensor_copy(
                 w2_dealt[:].rearrange("p a t (m e) -> p a t m e", e=2),
                 w2_raw[:].rearrange("p a (m t e) -> p a t m e", t=PACK, e=2),
             )
-            for h in range(HALVES):
-                pick(1, h)
+            pick(1)
             for a in range(PASSES):
                 dealt = w1_bf[a][:].rearrange("p t m j -> p m t j")
-                for half in range(2):
-                    raw = w1_raw[a][half][:].rearrange("p j (m t) -> p m t j", t=PACK)
-                    split = W1_SPLIT[a][half]
-                    if split > 0:
-                        nc.vector.tensor_copy(dealt[:, 64 * half:64 * half + split], raw[:, :split])
-                    if split < 64:
-                        nc.scalar.copy(dealt[:, 64 * half + split:64 * half + 64], raw[:, split:])
+                raw = w1_raw[a][:].rearrange("p j (m t) -> p m t j", t=PACK)
+                split = W1_ON_VECTOR[a]
+                nc.vector.tensor_copy(dealt[:, :split], raw[:, :split])
+                nc.scalar.copy(dealt[:, split:], raw[:, split:])
                 flat = w1_bf[a][:].rearrange("p t m j -> p (t m j)")
-                for lo, hi in ((0, 1), (1, 2), (2, 4)) if a == 1 else ((0, 4),):
+                for lo, hi in ((0, 1), (1, 2), (2, PACK)) if a == PASSES - 1 else ((0, PACK),):
                     nc.vector.quantize_mx(
-                        out=w1_codes[a][:, P * lo:P * hi].bitcast(FP8X4), scales=w1_scales[a][:, P * lo:P * hi],
-                        in_=flat[:, BANK * lo:BANK * hi],
+                        out=w1_codes[a][:, P * lo:P * hi].bitcast(FP8X4),
+                        scales=w1_scales[a][:, P * lo:P * hi],
+                        in_=flat[:, PASS * lo:PASS * hi],
                     )
 
         tail = ctx.enter_context(tc.tile_pool(name="tail", bufs=1))
-        x_pairs = [tail.tile([P, 2, BANK, 2], BF16, name="x_pairs_%d" % h, tag="x_pairs_%d" % h, align_bytes=64) for h in range(HALVES)]
+        page_pairs = [tail.tile([P, 2, BANK, 2], BF16, name="page_pairs_%d" % c) for c in range(CHUNKS)]
         page_codes = tail.tile([P, T2], I32, name="page_codes", align_bytes=64)
         page_scales = tail.tile([P, T2], U8, name="page_scales", align_bytes=64)
 
-        after, read = {}, {}
-        summed, cells_of = {}, {}
-        floored = {}
-        sums, tanh_of, third, prod = {}, {}, {}, {}
+        def product(w, t, h):
+            bank = psum.tile([P, BANK], F32, name="bank_%d" % w, bufs=BANK_BUFS[w])
+            for a in range(PASSES):
+                if w == 0:
+                    codes = w1_codes[a][:, P * t:P * (t + 1)].bitcast(FP8X4)
+                    scales = w1_scales[a][:, P * t:P * (t + 1)]
+                else:
+                    codes = w2_dealt[:, a, t, :].bitcast(FP4X4) if w == 1 else w3_dealt[:, a, t, :].bitcast(FP8X4)
+                    first = S + H * (w - 1) + P * t
+                    scales = given_scales[:, a, first:first + P]
+                nc.tensor.matmul_mx(
+                    out=bank[:], lhsT=codes, lhsT_scale=scales,
+                    rhs=picked[a][h][:].bitcast(FP8X4), rhs_scale=given_scales[:, a, half(h)],
+                    start=(a == 0), stop=(a == PASSES - 1),
+                )
+            return bank
 
-        def first_product(u):
-            sums[u] = []
-            products(u, (0,))
-
-        def other_products(u):
-            products(u, (1, 2))
-
-        def products(u, which):
-            t, h = divmod(u, HALVES)
-            cols = slice(P * t, P * (t + 1))
-            for w in which:
-                bank = psum.tile([P, BANK], F32, name="bank_%d" % w)
-                for a in range(PASSES):
-                    if w == 0:
-                        codes, scales = w1_codes[a][:, cols].bitcast(FP8X4), w1_scales[a][:, cols]
-                    elif w == 1:
-                        codes, scales = w2_dealt[:, a, t, :].bitcast(FP4X4), planes[:, a, S + P * t:S + P * (t + 1)]
-                    else:
-                        codes, scales = w3_dealt[:, a, t, :].bitcast(FP8X4), planes[:, a, S + H + P * t:S + H + P * (t + 1)]
-                    nc.tensor.matmul_mx(
-                        out=bank[:], lhsT=codes, lhsT_scale=scales,
-                        rhs=picked[a][h][:].bitcast(FP8X4), rhs_scale=planes[:, a, BANK * h:BANK * (h + 1)],
-                        start=(a == 0), stop=(a == PASSES - 1),
-                    )
-                sums[u].append(bank)
-
-        def work(name, slot, rows=1):
-            return keep.tile([P, rows, BANK], F32, name=name, tag=slot, align_bytes=64)
-
-        def diff_slot(t):
-            return "cells_%d" % (t - 1)
-
-        def even_slot(t):
-            return ("", "unit_5", "after_1", "summed_1")[t]
-
-        def copy_third(u):
-            third[u] = ring.tile([P, BANK], F32, name="third")
-            nc.scalar.copy(third[u][:], sums[u][2][:])
-
-        def add_hum(u):
-            if u < HALVES:
-                slot = "summed_%d" % u
-            elif u == 2:
-                slot = diff_slot(0)
-            elif u == 6:
-                slot = even_slot(1)
-            else:
-                slot = "unit_%d" % (u - 1)
-            summed[u] = work("summed_%d" % u, slot)[:, 0, :]
-            if u < HALVES:
-                nc.vector.tensor_tensor(summed[u], sums[u][0][:], hum_sb[u][:], ALU.add)
-            else:
-                first = ring.tile([P, BANK], F32, name="first", bufs=3)
-                nc.scalar.copy(first[:], sums[u][0][:])
-                nc.gpsimd.tensor_tensor(summed[u], first[:], hum_sb[u][:], ALU.add)
-
-        def tanh(u):
-            t, h = divmod(u, HALVES)
-            tanh_of[u] = work("tanh_%d" % u, ("after_%d" if h else "tanh_even_%d") % t)[:, 0, :]
-            nc.scalar.activation(tanh_of[u], summed[u], ACT.Tanh)
-
-        def multiply(u):
-            t, h = divmod(u, HALVES)
-            slot = "tanh_even_%d" % t if h and t else diff_slot(t)
-            if t == PACK - 1:
-                slot = diff_slot(t) if h else "after_%d" % (t - 1)
-            prod[u] = work("prod_%d" % u, slot)[:, 0, :]
-            if u != UNITS - 2:
-                nc.vector.tensor_tensor(prod[u], sums[u][1][:], tanh_of[u], ALU.mult)
-            else:
-                second = ring.tile([P, BANK], F32, name="first", bufs=3)
-                nc.scalar.copy(second[:], sums[u][1][:])
-                nc.gpsimd.tensor_tensor(prod[u], second[:], tanh_of[u], ALU.mult)
-            if h == 1 and t > 0:
-                after[t] = work("after_%d" % t, "after_%d" % t, 1 + HALVES)
-                read[t - 1] = after[t][:, 1:, :].rearrange("p h j -> p (h j)")
-
-        def combine(u):
-            t, h = divmod(u, HALVES)
-            cols = slice(BANK * h, BANK * (h + 1))
-            cells = work("cells_%d" % u, "cells_%d" % t if h else "summed_0")[:, 0, :] if h or t == 0 else after[t][:, 0, :]
-            if t == 0:
-                diff = prod[u] if h else work("diff_0", "tanh_even_0")[:, 0, :]
-                nc.vector.tensor_tensor(diff, prod[u], sums[u][2][:], ALU.subtract)
-            else:
-                diff = work("diff_%d" % u, even_slot(t))[:, 0, :]
-                nc.gpsimd.tensor_tensor(diff, prod[u], third[u][:], ALU.subtract)
-            nc.gpsimd.tensor_tensor(cells, diff, wgs_sb[t][:, cols], ALU.mult)
-            cells_of[u] = cells
-
-        def put(u):
-            t, h = divmod(u, HALVES)
-            nc.vector.tensor_copy(page[t][:].indirect(idx2[:, LIST_COLS * h:LIST_COLS * (h + 1)]), cells_of[u])
-
-        def read_page(t):
-            nc.sync.dma_start(out=page_out[t], in_=page[t][:])
-            nc.vector.tensor_copy(read[t], page[t][:].indirect(idx3[:]))
-
-        def floor_at_base(t):
-            floored[t] = work("floored_%d" % t, even_slot(t + 1) if t else "unit_%d" % (UNITS - 1), HALVES)
-            if True:
-                nc.gpsimd.tensor_scalar(floored[t][:].rearrange("p h j -> p (h j)"), read[t], F32_MAX, base_sb[:, t:t + 1], ALU.min, ALU.max)
-
-        def round_x(t):
+        def copied(w, t, tag):
+            values = row_tile("sum_%d_%d" % (w, t), tag)
             for h in range(HALVES):
-                nc.scalar.copy(x_pairs[h][:, t // 2, :, t % 2], floored[t][:, h, :])
+                nc.scalar.copy(values[:, half(h)], product(w, t, h)[:])
+            return values
+
+        def cells_of(t, h_rows, tag):
+            cells = row_tile("cells_%d" % t, tag)
+            nc.gpsimd.tensor_tensor(cells[:], h_rows[:], wgs_sb[t][:], ALU.mult)
+            return cells
+
+        def put(t, cells):
+            nc.vector.tensor_copy(page[t][:].indirect(idx2[:]), cells[:])
+            nc.sync.dma_start(out=page_out[t], in_=page[t][:])
+
+        def fetch(t):
+            read = row_tile("read_%d" % t, "read_%d" % t)
+            nc.vector.tensor_copy(read[:], page[t][:].indirect(idx3[:]))
+            return read
 
         def round_page(t):
             for c in range(CHUNKS):
-                nc.scalar.copy(page_pairs[c][:, t // 2, :, t % 2], page[t][:, BANK * c:BANK * (c + 1)])
+                nc.scalar.copy(page_pairs[c][:, t // 2, :, t % 2], page[t][:, half(c)])
 
-        def weave(pairs, slot):
-            woven = tail.tile([P, BANK * PACK], BF16, name="woven", tag=slot, align_bytes=64)
+        def weave(pairs, tag):
+            woven = keep.tile([P, BANK * PACK], BF16, name="woven", tag=tag, align_bytes=64)
             nc.vector.tensor_copy(
                 woven[:].bitcast(I32).rearrange("p (j u) -> p j u", u=2),
                 pairs[:].rearrange("p u j e -> p u (j e)").bitcast(I32).rearrange("p u j -> p j u"),
             )
             return woven
 
-        for u in range(HALVES):
-            first_product(u)
-            add_hum(u)
-            tanh(u)
-        w3_dealt = keep.tile([P, PASSES, PACK, P], I32, name="w3_dealt", tag="unit_0", align_bytes=64)
+        tanh_0 = row_tile("tanh_0", "tanh_0")
+        for h in range(HALVES):
+            nc.vector.tensor_tensor(tanh_0[:, half(h)], product(0, 0, h)[:], hum_first[h][:], ALU.add)
+            nc.scalar.activation(tanh_0[:, half(h)], tanh_0[:, half(h)], ACT.Tanh)
+        w3_dealt = keep.tile([P, PASSES, PACK, P], I32, name="w3_dealt", tag="hum_0_0", align_bytes=64)
         nc.vector.tensor_copy(
-            w3_dealt[:].rearrange("p a t m -> p a m t"),
-            w3_raw[:].rearrange("p a (m t) -> p a m t", t=PACK),
+            w3_dealt[:].rearrange("p a t m -> p a m t"), w3_raw[:].rearrange("p a (m t) -> p a m t", t=PACK)
         )
-        for u in range(HALVES):
-            other_products(u)
-        page_pairs = []
-        for t in range(PACK):
-            units = range(HALVES * t, HALVES * (t + 1))
-            if t == 0:
-                for u in units:
-                    multiply(u)
-                    combine(u)
-            else:
-                for u in units:
-                    multiply(u)
-                read_page(t - 1)
-                for u in units:
-                    combine(u)
-            for u in units:
-                put(u)
-            for u in range(HALVES * (t + 2) if t else HALVES, min(HALVES * (t + 3), UNITS)):
-                first_product(u)
-                add_hum(u)
-                tanh(u)
-            for u in range(HALVES * (t + 1), min(HALVES * (t + 2), UNITS)):
-                other_products(u)
-                copy_third(u)
-            if t == 1:
-                for c, slot in enumerate(("unit_2", "unit_3", "unit_4", "cells_0")):
-                    page_pairs.append(keep.tile([P, 2, BANK, 2], BF16, name="page_pairs_%d" % c, tag=slot, align_bytes=64))
-            if t > 0:
-                floor_at_base(t - 1)
-                round_page(t - 1)
-            if t == 0:
-                nc.scalar.copy(w4_bf[:], w4_raw[:].rearrange("p j n -> p n j"))
-            if t > 1:
-                round_x(t - 2)
-            if t == PACK - 1:
-                nc.scalar.activation(warm[:, 1:2], third[UNITS - 1][:, 0:1], ACT.Sqrt, bias=1.0, scale=0.0)
-        round_x(PACK - 2)
-        w4_codes = keep.tile([P, N], U32, name="w4_codes", tag="cells_%d" % (PACK - 1), align_bytes=64)
-        for lo, hi in ((0, 256), (256, N)):
+        first_2 = copied(0, 2, "first_2")
+        nc.gpsimd.tensor_tensor(first_2[:, half(0)], first_2[:, half(0)], hum_sb[2][:, half(0)], ALU.add)
+        tanh_1 = row_tile("tanh_1", "tanh_1")
+        h_0 = row_tile("h_0", "h_0")
+        cells_0 = row_tile("cells_0", "cells_0")
+        for h in range(HALVES):
+            nc.vector.tensor_tensor(h_0[:, half(h)], product(1, 0, h)[:], tanh_0[:, half(h)], ALU.mult)
+        for h in range(HALVES):
+            nc.vector.tensor_tensor(tanh_1[:, half(h)], product(0, 1, h)[:], hum_sb[1][:, half(h)], ALU.add)
+            nc.scalar.activation(tanh_1[:, half(h)], tanh_1[:, half(h)], ACT.Tanh)
+            nc.vector.tensor_tensor(h_0[:, half(h)], h_0[:, half(h)], product(2, 0, h)[:], ALU.subtract)
+            nc.gpsimd.tensor_tensor(cells_0[:, half(h)], h_0[:, half(h)], wgs_sb[0][:, half(h)], ALU.mult)
+        gated_1 = row_tile("gated_1", "tanh_0")
+        for h in range(HALVES):
+            nc.vector.tensor_tensor(gated_1[:, half(h)], product(1, 1, h)[:], tanh_1[:, half(h)], ALU.mult)
+        third_1 = copied(2, 1, "third_1")
+
+        tanh_2 = row_tile("tanh_2", "h_0")
+        nc.gpsimd.tensor_tensor(tanh_2[:, half(1)], first_2[:, half(1)], hum_sb[2][:, half(1)], ALU.add)
+        nc.scalar.activation(tanh_2[:, half(0)], first_2[:, half(0)], ACT.Tanh)
+        nc.scalar.activation(tanh_2[:, half(1)], tanh_2[:, half(1)], ACT.Tanh)
+        h_1 = row_tile("h_1", "hum_2")
+        nc.gpsimd.tensor_tensor(h_1[:], gated_1[:], third_1[:], ALU.subtract)
+        cells_1 = cells_of(1, h_1, "third_1")
+        put(0, cells_0)
+        read = [fetch(0)]
+
+        first_3 = copied(0, 3, "hum_1")
+        sums = {t: (copied(1, t, "second_%d" % t), copied(2, t, "third_%d" % t)) for t in (2, 3)}
+        round_page(0)
+        tanh_3 = row_tile("tanh_3", "hum_2")
+        nc.gpsimd.tensor_tensor(tanh_3[:], first_3[:], hum_sb[3][:], ALU.add)
+        nc.scalar.activation(tanh_3[:], tanh_3[:], ACT.Tanh)
+        cells = {1: cells_1}
+        for t, tanh_t in ((2, tanh_2), (3, tanh_3)):
+            second, third = sums[t]
+            h_t = row_tile("h_%d" % t, "hum_3")
+            nc.gpsimd.tensor_tensor(h_t[:], second[:], tanh_t[:], ALU.mult)
+            nc.gpsimd.tensor_tensor(h_t[:], h_t[:], third[:], ALU.subtract)
+            cells[t] = cells_of(t, h_t, "third_%d" % t)
+        nc.scalar.activation(warm[:, 1:2], tanh_3[:, 0:1], ACT.Sqrt, bias=1.0, scale=0.0)
+        nc.scalar.copy(w4_bf[:], w4_raw[:].rearrange("p j n -> p n j"))
+        for t in range(1, PACK - 1):
+            put(t, cells[t])
+            read.append(fetch(t))
+            round_page(t)
+        put(PACK - 1, cells[PACK - 1])
+
+        x_tags = ("hum_3", "wgs_3")
+        x_pairs = [
+            keep.tile([P, 2, BANK, 2], BF16, name="x_pairs_%d" % h, tag=x_tags[h], align_bytes=64)
+            for h in range(HALVES)
+        ]
+        for t in range(PACK - 1):
+            for h in range(HALVES):
+                nc.gpsimd.tensor_scalar(
+                    x_pairs[h][:, t // 2, :, t % 2], read[t][:, half(h)], F32_MAX, base_sb[:, t:t + 1], ALU.min, ALU.max
+                )
+
+        w4_codes = keep.tile([P, N], U32, name="w4_codes", tag="third_%d" % (PACK - 1), align_bytes=64)
+        for lo, hi in ((0, 2 * P), (2 * P, N)):
             nc.vector.quantize_mx(
                 out=w4_codes[:, lo:hi].bitcast(FP8X4), scales=w4_scales[:, lo:hi],
                 in_=w4_bf[:, lo:hi, :].rearrange("p n j -> p (n j)"),
             )
-        nc.sync.dma_start(out=page_out[PACK - 1], in_=page[PACK - 1][:])
         round_page(PACK - 1)
 
         for h in range(HALVES):
-            if h == 0:
-                last = work("read_last_0", even_slot(PACK - 1))[:, 0, :]
-            else:
-                last = tail.tile([P, BANK], F32, name="read_last_1", tag="x_pairs_0", align_bytes=64)[:]
-            nc.vector.tensor_copy(last, page[PACK - 1][:].indirect(idx3[:, LIST_COLS * h:LIST_COLS * (h + 1)]))
-            nc.vector.tensor_scalar(x_pairs[h][:, 1, :, 1], last, base_sb[:, PACK - 1:PACK], None, ALU.max)
-            woven = weave(x_pairs[h], "woven" if h else "x_first")
+            tag = x_tags[0] if h else "read_%d" % (PACK - 2)
+            last = keep.tile([P, BANK], F32, name="read_last_%d" % h, tag=tag, align_bytes=64)
+            nc.vector.tensor_copy(last[:], page[PACK - 1][:].indirect(entries(idx3, h)))
+            nc.vector.tensor_scalar(x_pairs[h][:, 1, :, 1], last[:], base_sb[:, PACK - 1:PACK], None, ALU.max)
+            woven = weave(x_pairs[h], "second_%d" % (2 + h))
             x_codes = tail.tile([P, BANK], U32, name="x_codes_%d" % h, align_bytes=64)
             x_scales = tail.tile([P, BANK], U8, name="x_scales_%d" % h, align_bytes=64)
             nc.vector.quantize_mx(out=x_codes[:].bitcast(FP8X4), scales=x_scales[:], in_=woven[:])
-            size = work("size_%d" % h, "after_%d" % h, N // P)
-            root = work("root_%d" % h, "after_%d" % (3 - h), N // P)
+            scores = tail.tile([P, N // P, BANK], F32, name="scores_%d" % h)
             for n in range(N // P):
                 cols = slice(P * n, P * (n + 1))
-                score = psum.tile([P, BANK], F32, name="bank_%d" % n)
+                bank = psum.tile([P, BANK], F32, name="bank_%d" % n, bufs=BANK_BUFS[n])
                 nc.tensor.matmul_mx(
-                    out=score[:], lhsT=w4_codes[:, cols].bitcast(FP8X4), lhsT_scale=w4_scales[:, cols],
+                    out=bank[:], lhsT=w4_codes[:, cols].bitcast(FP8X4), lhsT_scale=w4_scales[:, cols],
                     rhs=x_codes[:].bitcast(FP8X4), rhs_scale=x_scales[:], start=True, stop=True,
                 )
-                nc.scalar.activation(size[:, n, :], score[:], ACT.Abs)
-            for lo, hi in ((0, 2), (2, 3)) if h else ((0, 3),):
-                nc.scalar.activation(root[:, lo:hi, :], size[:, lo:hi, :], ACT.Sqrt, bias=1.0)
-                nc.scalar.dma_start(out=scores_out[:, lo:hi, BANK * h:BANK * (h + 1)], in_=root[:, lo:hi, :])
+                nc.scalar.activation(scores[:, n, :], bank[:], ACT.Abs)
+            for lo, hi in ((0, 2), (2, 3)) if h == HALVES - 1 else ((0, 3),):
+                nc.scalar.activation(scores[:, lo:hi, :], scores[:, lo:hi, :], ACT.Sqrt, bias=1.0)
+                nc.scalar.dma_start(out=scores_out[:, lo:hi, half(h)], in_=scores[:, lo:hi, :])
 
-        words_out = out_2[0].rearrange("p m i -> p (m i)").bitcast(I32)
-        for c in range(CHUNKS):
-            cols = slice(BANK * c, BANK * (c + 1))
-            woven = weave(page_pairs[c], ("x_pairs_0", "x_first", "x_pairs_1", "woven")[c])
-            nc.vector.quantize_mx(out=page_codes[:, cols].bitcast(FP8X4), scales=page_scales[:, cols], in_=woven[:])
+        for c, tag in enumerate((x_tags[0], "second_2", x_tags[1], "second_3")):
+            woven = weave(page_pairs[c], tag)
+            nc.vector.quantize_mx(
+                out=page_codes[:, half(c)].bitcast(FP8X4), scales=page_scales[:, half(c)], in_=woven[:]
+            )
             if c > 0:
-                both = slice(BANK * (c - 1), BANK * (c + 1)) if c == 1 else cols
-                nc.sync.dma_start(out=words_out[:, both], in_=page_codes[:, both])
-        for quad in range(4):
-            (nc.gpsimd if quad % 2 else nc.sync).dma_start(
+                cols = slice(0, 2 * BANK) if c == 1 else half(c)
+                nc.sync.dma_start(out=words_out[:, cols], in_=page_codes[:, cols])
+        for quad in range(QUADS):
+            nc.sync.dma_start(
                 out=out_3[0, 4 * quad:4 * quad + 4, :].bitcast(I32),
                 in_=page_scales[32 * quad:32 * quad + 4, :].bitcast(I32),
             )

from contextlib import ExitStack

import concourse.mybir as mybir

K, T, S, H, T2, NREAD, N = 1024, 4096, 1024, 512, 2048, 1024, 384
FLOPS = 2 * (3 * K * H * S + H * N * NREAD)

F32 = mybir.dt.float32
BF16 = mybir.dt.bfloat16
I32 = mybir.dt.int32
U32 = mybir.dt.uint32
U16 = mybir.dt.uint16
U8 = mybir.dt.uint8
FP8X4 = mybir.dt.float8_e4m3fn_x4
FP4X4 = mybir.dt.float4_e2m1fn_x4
ALU = mybir.AluOpType
ACT = mybir.ActivationFunctionType

P = 128
PACK = 4
PASS = P * PACK
PASSES = K // PASS
BLOCKS = PASS // 32
QUADS = 4
BANK = 512
HALVES = S // BANK
CHUNKS = T2 // BANK
LIST_COLS = BANK // 16
F32_MAX = 3.4028234663852886e38
BANK_BUFS = (4, 2, 2)
W1_ON_VECTOR = (76, 84)
QUAD_ORDER = (0, 2, 1, 3)


def tile_list_arrester_varistor_page_kernel(
    tc, tab_words, tab_scales, offs, offs2, offs3, w1, w2_words, w2_scales,
    w3_words, w3_scales, hum, wgs, page0, base, w4, out_0, out_1, out_2, out_3,
):
    nc = tc.nc
    hum_rows = hum.rearrange("(p t) j -> t p j", t=PACK)
    wgs_rows = wgs.rearrange("(q t) j -> t q j", t=PACK)
    page_in = page0.rearrange("(p t) c -> t p c", t=PACK)
    page_out = out_1.rearrange("(p t) c -> t p c", t=PACK)
    scores_out = out_0.rearrange("(n p) m -> p n m", p=P)
    words_out = out_2[0].rearrange("p m i -> p (m i)").bitcast(I32)

    def half(h):
        return slice(BANK * h, BANK * (h + 1))

    def entries(offsets, h):
        return offsets[:, LIST_COLS * h:LIST_COLS * (h + 1)]

    with ExitStack() as ctx:
        lists = ctx.enter_context(tc.tile_pool(name="lists", bufs=1))
        keep = ctx.enter_context(tc.tile_pool(name="keep", bufs=1))
        psum = ctx.enter_context(tc.psum_pool(name="psum", bufs=2))

        def row_tile(name, tag):
            return keep.tile([P, S], F32, name=name, tag=tag, align_bytes=64)

        idx1 = lists.tile([P, S // 16], U16, name="idx1")
        idx2 = lists.tile([P, S // 16], U16, name="idx2")
        idx3 = lists.tile([P, NREAD // 16], U16, name="idx3")

        given_scales = keep.tile([P, PASSES, S + 2 * H], U8, name="given_scales", align_bytes=64)
        picked = [
            [keep.tile([P, BANK], I32, name="picked_%d_%d" % (a, h), align_bytes=64) for h in range(HALVES)]
            for a in range(PASSES)
        ]
        w1_codes = [keep.tile([P, H], U32, name="w1_codes_%d" % a, align_bytes=64) for a in range(PASSES)]
        w1_scales = [keep.tile([P, H], U8, name="w1_scales_%d" % a, align_bytes=64) for a in range(PASSES)]
        w2_dealt = keep.tile([P, PASSES, PACK, 2 * P], U8, name="w2_dealt", align_bytes=64)
        w3_raw = keep.tile([P, PASSES, H], I32, name="w3_raw")
        hum_first = [
            keep.tile([P, BANK], F32, name="hum_0_%d" % h, tag="hum_0_%d" % h, align_bytes=64) for h in range(HALVES)
        ]
        hum_sb = {t: row_tile("hum_%d" % t, "hum_%d" % t) for t in range(1, PACK)}
        wgs_sb = [row_tile("wgs_%d" % t, "wgs_%d" % t) for t in range(PACK)]
        page = [keep.tile([P, T2], F32, name="page_%d" % t) for t in range(PACK)]
        base_sb = keep.tile([P, PACK], F32, name="base_sb")
        w4_raw = keep.tile([P, PACK, N], F32, name="w4_raw")
        w4_bf = keep.tile([P, N, PACK], BF16, name="w4_bf", align_bytes=64)
        w4_scales = keep.tile([P, N], U8, name="w4_scales", align_bytes=64)

        warm = keep.tile([P, 2], F32, name="warm")
        nc.vector.memset(warm[:, 0:1], 0.0)
        nc.scalar.activation(warm[:, 1:2], warm[:, 0:1], ACT.Tanh)

        def load_wgs(t):
            for quad in QUAD_ORDER:
                nc.sync.dma_start(out=wgs_sb[t][32 * quad:32 * quad + 32, :], in_=wgs_rows[t])

        with tc.tile_pool(name="head", bufs=1) as head:
            table = [head.tile([P, T], I32, name="table_%d" % a) for a in range(PASSES)]
            tab_rows = head.tile([P, T], U8, name="tab_rows")
            picked_rows = head.tile([P, S], U8, name="picked_rows")
            w_rows = head.tile([P, 2, H], U8, name="w_rows")
            staged = head.tile([P, S + 2 * H], U8, name="staged")
            w1_raw = [head.tile([P, PACK, H], F32, name="w1_raw_%d" % a) for a in range(PASSES)]
            w1_bf = [
                head.tile([P, PACK, P, PACK], BF16, name="w1_bf_%d" % a, align_bytes=64) for a in range(PASSES)
            ]
            w2_raw = head.tile([P, PASSES, 2 * H], U8, name="w2_raw")

            rows = PASSES * BLOCKS
            for lo, hi in ((rows, 64), (64, P)):
                nc.vector.memset(tab_rows[lo:hi, :].bitcast(I32), 0)
                nc.vector.memset(w_rows[lo:hi].rearrange("p w c -> p (w c)").bitcast(I32), 0)
            nc.vector.memset(given_scales[:].rearrange("p a c -> p (a c)").bitcast(I32), 0)

            nc.sync.dma_start(idx1[:], offs)
            nc.sync.dma_start(
                out=tab_rows[0:rows, :].bitcast(I32), in_=tab_scales.rearrange("a q n -> (a q) n").bitcast(I32)
            )
            for w, scales in enumerate((w2_scales, w3_scales)):
                nc.sync.dma_start(
                    out=w_rows[0:rows, w, :].bitcast(I32), in_=scales.rearrange("a q c -> (a q) c").bitcast(I32)
                )
            nc.sync.dma_start(out=table[0][:], in_=tab_words[0].rearrange("p n i -> p (n i)").bitcast(I32))
            nc.sync.dma_start(out=w2_raw[:].bitcast(I32), in_=w2_words.rearrange("a p c -> p a c").bitcast(I32))
            nc.sync.dma_start(out=table[1][:], in_=tab_words[1].rearrange("p n i -> p (n i)").bitcast(I32))
            for a in range(PASSES):
                nc.sync.dma_start(
                    out=w1_raw[a][:], in_=w1[PASS * a:PASS * (a + 1), :].rearrange("(p j) c -> p j c", j=PACK)
                )
            nc.sync.dma_start(out=hum_first[0][:], in_=hum_rows[0][:, half(0)])
            nc.sync.dma_start(out=w3_raw[:], in_=w3_words.rearrange("a p c i -> p a (c i)").bitcast(I32))
            nc.sync.dma_start(out=hum_first[1][:], in_=hum_rows[0][:, half(1)])
            nc.sync.dma_start(out=hum_sb[1][:], in_=hum_rows[1])
            nc.sync.dma_start(out=hum_sb[2][:], in_=hum_rows[2])
            load_wgs(0)
            nc.sync.dma_start(out=page[0][:], in_=page_in[0])
            nc.sync.dma_start(idx2[:], offs2)
            nc.sync.dma_start(out=hum_sb[3][:], in_=hum_rows[3])
            nc.sync.dma_start(idx3[:], offs3)
            nc.sync.dma_start(out=base_sb[:], in_=base.rearrange("(p t) -> p t", t=PACK))
            load_wgs(1)
            nc.sync.dma_start(out=page[1][:], in_=page_in[1])
            nc.sync.dma_start(out=w4_raw[:], in_=w4.rearrange("(p j) n -> p j n", j=PACK))
            for t in range(2, PACK):
                load_wgs(t)
                nc.sync.dma_start(out=page[t][:], in_=page_in[t])

            nc.vector.tensor_copy(picked_rows[:], tab_rows[:].indirect(idx1[:]))
            nc.vector.tensor_copy(staged[:, 0:S].bitcast(I32), picked_rows[:].bitcast(I32))
            nc.vector.tensor_copy(
                staged[:, S:].rearrange("p (w t m) -> p w t m", w=2, t=PACK),
                w_rows[:].rearrange("p w (m t) -> p w t m", t=PACK),
            )
            for a in range(PASSES):
                for quad in range(QUADS):
                    row = BLOCKS * a + 4 * quad
                    (nc.scalar if a else nc.gpsimd).dma_start(
                        out=given_scales[32 * quad:32 * quad + 4, a, :].bitcast(I32),
                        in_=staged[row:row + 4, :].bitcast(I32),
                    )

            def pick(a):
                for h in range(HALVES):
                    nc.vector.tensor_copy(
                        picked[a][h][:].bitcast(U32), table[a][:].bitcast(U32).indirect(entries(idx1, h))
                    )

            pick(0)
            nc.vector.tensor_copy(
                w2_dealt[:].rearrange("p a t (m e) -> p a t m e", e=2),
                w2_raw[:].rearrange("p a (m t e) -> p a t m e", t=PACK, e=2),
            )
            pick(1)
            for a in range(PASSES):
                dealt = w1_bf[a][:].rearrange("p t m j -> p m t j")
                raw = w1_raw[a][:].rearrange("p j (m t) -> p m t j", t=PACK)
                split = W1_ON_VECTOR[a]
                nc.vector.tensor_copy(dealt[:, :split], raw[:, :split])
                nc.scalar.copy(dealt[:, split:], raw[:, split:])
                flat = w1_bf[a][:].rearrange("p t m j -> p (t m j)")
                for lo, hi in ((0, 1), (1, 2), (2, PACK)) if a == PASSES - 1 else ((0, PACK),):
                    nc.vector.quantize_mx(
                        out=w1_codes[a][:, P * lo:P * hi].bitcast(FP8X4),
                        scales=w1_scales[a][:, P * lo:P * hi],
                        in_=flat[:, PASS * lo:PASS * hi],
                    )

        tail = ctx.enter_context(tc.tile_pool(name="tail", bufs=1))
        page_pairs = [tail.tile([P, 2, BANK, 2], BF16, name="page_pairs_%d" % c) for c in range(CHUNKS)]
        page_codes = tail.tile([P, T2], I32, name="page_codes", align_bytes=64)
        page_scales = tail.tile([P, T2], U8, name="page_scales", align_bytes=64)

        def product(w, t, h):
            bank = psum.tile([P, BANK], F32, name="bank_%d" % w, bufs=BANK_BUFS[w])
            for a in range(PASSES):
                if w == 0:
                    codes = w1_codes[a][:, P * t:P * (t + 1)].bitcast(FP8X4)
                    scales = w1_scales[a][:, P * t:P * (t + 1)]
                else:
                    codes = w2_dealt[:, a, t, :].bitcast(FP4X4) if w == 1 else w3_dealt[:, a, t, :].bitcast(FP8X4)
                    first = S + H * (w - 1) + P * t
                    scales = given_scales[:, a, first:first + P]
                nc.tensor.matmul_mx(
                    out=bank[:], lhsT=codes, lhsT_scale=scales,
                    rhs=picked[a][h][:].bitcast(FP8X4), rhs_scale=given_scales[:, a, half(h)],
                    start=(a == 0), stop=(a == PASSES - 1),
                )
            return bank

        def copied(w, t, tag):
            values = row_tile("sum_%d_%d" % (w, t), tag)
            for h in range(HALVES):
                nc.scalar.copy(values[:, half(h)], product(w, t, h)[:])
            return values

        def cells_of(t, h_rows, tag):
            cells = row_tile("cells_%d" % t, tag)
            nc.gpsimd.tensor_tensor(cells[:], h_rows[:], wgs_sb[t][:], ALU.mult)
            return cells

        def put(t, cells):
            nc.vector.tensor_copy(page[t][:].indirect(idx2[:]), cells[:])
            nc.sync.dma_start(out=page_out[t], in_=page[t][:])

        def fetch(t):
            read = row_tile("read_%d" % t, "read_%d" % t)
            nc.vector.tensor_copy(read[:], page[t][:].indirect(idx3[:]))
            return read

        def round_page(t):
            for c in range(CHUNKS):
                nc.scalar.copy(page_pairs[c][:, t // 2, :, t % 2], page[t][:, half(c)])

        def weave(pairs, tag):
            woven = keep.tile([P, BANK * PACK], BF16, name="woven", tag=tag, align_bytes=64)
            nc.vector.tensor_copy(
                woven[:].bitcast(I32).rearrange("p (j u) -> p j u", u=2),
                pairs[:].rearrange("p u j e -> p u (j e)").bitcast(I32).rearrange("p u j -> p j u"),
            )
            return woven

        tanh_0 = row_tile("tanh_0", "tanh_0")
        for h in range(HALVES):
            nc.vector.tensor_tensor(tanh_0[:, half(h)], product(0, 0, h)[:], hum_first[h][:], ALU.add)
            nc.scalar.activation(tanh_0[:, half(h)], tanh_0[:, half(h)], ACT.Tanh)
        w3_dealt = keep.tile([P, PASSES, PACK, P], I32, name="w3_dealt", tag="hum_0_0", align_bytes=64)
        nc.vector.tensor_copy(
            w3_dealt[:].rearrange("p a t m -> p a m t"), w3_raw[:].rearrange("p a (m t) -> p a m t", t=PACK)
        )
        first_2 = copied(0, 2, "first_2")
        nc.gpsimd.tensor_tensor(first_2[:, half(0)], first_2[:, half(0)], hum_sb[2][:, half(0)], ALU.add)
        tanh_1 = row_tile("tanh_1", "tanh_1")
        h_0 = row_tile("h_0", "h_0")
        cells_0 = row_tile("cells_0", "cells_0")
        for h in range(HALVES):
            nc.vector.tensor_tensor(h_0[:, half(h)], product(1, 0, h)[:], tanh_0[:, half(h)], ALU.mult)
        for h in range(HALVES):
            nc.vector.tensor_tensor(tanh_1[:, half(h)], product(0, 1, h)[:], hum_sb[1][:, half(h)], ALU.add)
            nc.scalar.activation(tanh_1[:, half(h)], tanh_1[:, half(h)], ACT.Tanh)
            nc.vector.tensor_tensor(h_0[:, half(h)], h_0[:, half(h)], product(2, 0, h)[:], ALU.subtract)
            nc.gpsimd.tensor_tensor(cells_0[:, half(h)], h_0[:, half(h)], wgs_sb[0][:, half(h)], ALU.mult)
        gated_1 = row_tile("gated_1", "tanh_0")
        for h in range(HALVES):
            nc.vector.tensor_tensor(gated_1[:, half(h)], product(1, 1, h)[:], tanh_1[:, half(h)], ALU.mult)
        third_1 = copied(2, 1, "third_1")

        tanh_2 = row_tile("tanh_2", "h_0")
        nc.gpsimd.tensor_tensor(tanh_2[:, half(1)], first_2[:, half(1)], hum_sb[2][:, half(1)], ALU.add)
        nc.scalar.activation(tanh_2[:, half(0)], first_2[:, half(0)], ACT.Tanh)
        nc.scalar.activation(tanh_2[:, half(1)], tanh_2[:, half(1)], ACT.Tanh)
        h_1 = row_tile("h_1", "hum_2")
        nc.gpsimd.tensor_tensor(h_1[:], gated_1[:], third_1[:], ALU.subtract)
        cells_1 = cells_of(1, h_1, "third_1")
        put(0, cells_0)
        read = [fetch(0)]

        first_3 = copied(0, 3, "hum_1")
        sums = {t: (copied(1, t, "second_%d" % t), copied(2, t, "third_%d" % t)) for t in (2, 3)}
        round_page(0)
        tanh_3 = row_tile("tanh_3", "hum_2")
        nc.gpsimd.tensor_tensor(tanh_3[:], first_3[:], hum_sb[3][:], ALU.add)
        nc.scalar.activation(tanh_3[:], tanh_3[:], ACT.Tanh)
        cells = {1: cells_1}
        for t, tanh_t in ((2, tanh_2), (3, tanh_3)):
            second, third = sums[t]
            h_t = row_tile("h_%d" % t, "hum_3")
            nc.gpsimd.tensor_tensor(h_t[:], second[:], tanh_t[:], ALU.mult)
            nc.gpsimd.tensor_tensor(h_t[:], h_t[:], third[:], ALU.subtract)
            cells[t] = cells_of(t, h_t, "third_%d" % t)
        nc.scalar.activation(warm[:, 1:2], tanh_3[:, 0:1], ACT.Sqrt, bias=1.0, scale=0.0)
        nc.scalar.copy(w4_bf[:], w4_raw[:].rearrange("p j n -> p n j"))
        for t in range(1, PACK - 1):
            put(t, cells[t])
            read.append(fetch(t))
            round_page(t)
        put(PACK - 1, cells[PACK - 1])

        x_tags = ("hum_3", "wgs_3")
        x_pairs = [
            keep.tile([P, 2, BANK, 2], BF16, name="x_pairs_%d" % h, tag=x_tags[h], align_bytes=64)
            for h in range(HALVES)
        ]
        for t in range(PACK - 1):
            for h in range(HALVES):
                nc.gpsimd.tensor_scalar(
                    x_pairs[h][:, t // 2, :, t % 2], read[t][:, half(h)], F32_MAX, base_sb[:, t:t + 1], ALU.min, ALU.max
                )

        w4_codes = keep.tile([P, N], U32, name="w4_codes", tag="third_%d" % (PACK - 1), align_bytes=64)
        for lo, hi in ((0, 2 * P), (2 * P, N)):
            nc.vector.quantize_mx(
                out=w4_codes[:, lo:hi].bitcast(FP8X4), scales=w4_scales[:, lo:hi],
                in_=w4_bf[:, lo:hi, :].rearrange("p n j -> p (n j)"),
            )
        round_page(PACK - 1)

        for h in range(HALVES):
            tag = x_tags[0] if h else "read_%d" % (PACK - 2)
            last = keep.tile([P, BANK], F32, name="read_last_%d" % h, tag=tag, align_bytes=64)
            nc.vector.tensor_copy(last[:], page[PACK - 1][:].indirect(entries(idx3, h)))
            nc.vector.tensor_scalar(x_pairs[h][:, 1, :, 1], last[:], base_sb[:, PACK - 1:PACK], None, ALU.max)
            woven = weave(x_pairs[h], "second_%d" % (2 + h))
            x_codes = tail.tile([P, BANK], U32, name="x_codes_%d" % h, align_bytes=64)
            x_scales = tail.tile([P, BANK], U8, name="x_scales_%d" % h, align_bytes=64)
            nc.vector.quantize_mx(out=x_codes[:].bitcast(FP8X4), scales=x_scales[:], in_=woven[:])
            scores = tail.tile([P, N // P, BANK], F32, name="scores_%d" % h)
            for n in range(N // P):
                cols = slice(P * n, P * (n + 1))
                bank = psum.tile([P, BANK], F32, name="bank_%d" % n, bufs=BANK_BUFS[n])
                nc.tensor.matmul_mx(
                    out=bank[:], lhsT=w4_codes[:, cols].bitcast(FP8X4), lhsT_scale=w4_scales[:, cols],
                    rhs=x_codes[:].bitcast(FP8X4), rhs_scale=x_scales[:], start=True, stop=True,
                )
                nc.scalar.activation(scores[:, n, :], bank[:], ACT.Abs)
            for lo, hi in ((0, 2), (2, 3)) if h == HALVES - 1 else ((0, 3),):
                nc.scalar.activation(scores[:, lo:hi, :], scores[:, lo:hi, :], ACT.Sqrt, bias=1.0)
                nc.scalar.dma_start(out=scores_out[:, lo:hi, half(h)], in_=scores[:, lo:hi, :])

        for c, tag in enumerate((x_tags[0], "second_2", x_tags[1], "second_3")):
            woven = weave(page_pairs[c], tag)
            nc.vector.quantize_mx(
                out=page_codes[:, half(c)].bitcast(FP8X4), scales=page_scales[:, half(c)], in_=woven[:]
            )
            if c > 0:
                cols = slice(0, 2 * BANK) if c == 1 else half(c)
                nc.sync.dma_start(out=words_out[:, cols], in_=page_codes[:, cols])
        for quad in range(QUADS):
            nc.sync.dma_start(
                out=out_3[0, 4 * quad:4 * quad + 4, :].bitcast(I32),
                in_=page_scales[32 * quad:32 * quad + 4, :].bitcast(I32),
            )
